import numpy as np
import ml_dtypes


def mxq(x, axis, fmt="e4m3"):
    dtype, down = {"e4m3": (ml_dtypes.float8_e4m3fn, 7), "e5m2": (ml_dtypes.float8_e5m2, 14)}[fmt]
    v = np.moveaxis(np.asarray(x, np.float32).astype(ml_dtypes.bfloat16).astype(np.float64), axis, -1)
    blocks = v.reshape(v.shape[:-1] + (-1, 32))
    amax = np.abs(blocks).max(-1, keepdims=True)
    byte = np.maximum(np.where(amax > 0, np.frexp(amax)[1] - 1 + 127, 0) - down, 1)
    scale = np.exp2(byte - 127.0)
    codes = (blocks / scale).astype(np.float32).astype(dtype).astype(np.float64)
    return np.moveaxis((codes * scale).reshape(v.shape), -1, axis)


WIDE = False


def mx_kscale(k):
    if not WIDE:
        return np.ones(k)
    levels = np.array([10, -10, 5, -5, 0])
    if k % 512:
        return np.exp2(np.random.permutation(np.resize(levels, k // 32))).repeat(32)
    a = np.empty((k // 512, 16))
    for p in range(k // 512):
        a[p, :8] = np.random.permutation(np.resize(levels, 8))
        for g in range(8):
            far = levels[np.abs(levels - a[p, g]) >= 10]
            a[p, g + 8] = far[np.random.randint(len(far))]
    return np.exp2(a.ravel()).repeat(32)


BF16 = ml_dtypes.bfloat16


def bf(x):
    return np.asarray(x, np.float32).astype(BF16)


def f64(x):
    return np.asarray(x).astype(np.float64)


E2M1 = np.array([0.0, 0.5, 1.0, 1.5, 2.0, 3.0, 4.0, 6.0, -0.0, -0.5, -1.0, -1.5, -2.0, -3.0, -4.0, -6.0])


def pack_weight(w, fmt):
    k, n = w.shape
    w = f64(bf(w)).reshape(k // 32, 32, n)
    amax = np.abs(w).max(1)
    if fmt == "e4m3":
        byte = np.frexp(amax)[1] - 1 + 127 - 7
    else:
        mant, ex = np.frexp(amax / 6.0)
        byte = np.where(mant > 0.5, ex, ex - 1) + 127
    byte = np.clip(np.where(amax > 0, byte, 1), 1, 254)
    scaled = (w * np.exp2(127.0 - byte)[:, None, :]).reshape(k, n).astype(np.float32)
    by_word = np.ascontiguousarray(scaled.reshape(k // 512, 128, 4, n).transpose(0, 1, 3, 2))
    if fmt == "e4m3":
        words = by_word.astype(ml_dtypes.float8_e4m3fn).view(np.uint8)
    else:
        c = by_word.astype(ml_dtypes.float4_e2m1fn).view(np.uint8) & 0xF
        words = c[..., 0::2] | (c[..., 1::2] << 4)
    return np.ascontiguousarray(words), np.ascontiguousarray(byte.astype(np.uint8).reshape(k // 512, 16, n))


def unpack_weight(words, scales, fmt):
    g, p, n, _ = words.shape
    if fmt == "e4m3":
        vals = np.ascontiguousarray(words).view(ml_dtypes.float8_e4m3fn).astype(np.float64)
    else:
        nib = np.empty((g, p, n, 4), np.uint8)
        nib[..., 0::2] = words & 0xF
        nib[..., 1::2] = words >> 4
        vals = E2M1[nib]
    vals = vals * np.repeat(np.exp2(scales.astype(np.float64) - 127.0), 8, axis=1)[..., None]
    return vals.transpose(0, 1, 3, 2).reshape(g * 512, n)
def pack4(w):
    words, scales = pack_weight(w, "e2m1")
    return words.reshape(words.shape[0], 128, -1), scales


def unpack4(words, scales):
    return unpack_weight(words.reshape(words.shape[0], 128, -1, 2), scales, "e2m1")


N, F, D, M = 1024, 1024, 1024, 1024


def draw0():
    p, q = mx_kscale(F), mx_kscale(D)
    x = bf(np.random.standard_normal((N, F)) * p)
    w_words, w_scales = pack4(np.random.standard_normal((F, D)) / np.sqrt(F) / p[:, None])
    c = bf(0.5 * np.random.standard_normal(D))
    g = bf((1.0 + 0.1 * np.random.standard_normal(D)) * q)
    a_words, a_scales = pack4(1.5 * np.random.standard_normal((D, M)) / np.sqrt(D) / q[:, None])
    s = bf(np.random.uniform(0.5, 2.0, M))
    return {"x": x, "w_words": w_words, "w_scales": w_scales, "c": c, "g": g, "a_words": a_words, "a_scales": a_scales, "s": s}


def _embed(x, w_words, w_scales, c, g):
    h = mxq(f64(x), 1, "e4m3") @ unpack4(w_words, w_scales)
    return np.tanh(h + f64(c)[None, :]) * f64(g)[None, :]


def core(x, w_words, w_scales, c, g, a_words, a_scales, s):
    z = _embed(x, w_words, w_scales, c, g)
    t = mxq(z, 1, "e4m3") @ unpack4(a_words, a_scales)
    sk = f64(s)
    u = sk[None, :] * t
    cos_u = np.cos(u)
    sin_u = np.sin(u)
    mc = np.mean(cos_u, axis=0)
    ms = np.mean(sin_u, axis=0)
    psi = np.exp(-sk * sk / 2.0)
    return 4.0 * sk[None, :] * (ms[None, :] * cos_u - (mc - psi)[None, :] * sin_u)


def e4m3fn_bytes(y):
    return np.clip(np.asarray(y, np.float64), -448.0, 448.0).astype(np.float32).astype(ml_dtypes.float8_e4m3fn).view(np.uint8)


def e4m3fn_values(b):
    return np.asarray(b, np.uint8).view(ml_dtypes.float8_e4m3fn).astype(np.float64)


def setup_inputs():
    d = draw0()
    x0 = np.asarray(d['x']).astype(np.float64)
    s = (np.max(np.abs(x0), axis=(0,), keepdims=True) / 448.0).astype(np.float32)
    out = {}
    for k, v in d.items():
        if k == 'x':
            out['x_bytes'] = e4m3fn_bytes(x0 / s.astype(np.float64))
            out['x_scale'] = s
        else:
            out[k] = v
    return out


def reference(x_bytes, x_scale, w_words, w_scales, c, g, a_words, a_scales, s):
    return core(e4m3fn_values(x_bytes) * x_scale.astype(np.float64), w_words, w_scales, c, g, a_words, a_scales, s)

@@ -1,0 +1,301 @@
+from contextlib import ExitStack
+import math
+
+import concourse.mybir as mybir
+from concourse.masks import make_identity
+
+F32 = mybir.dt.float32
+BF16 = mybir.dt.bfloat16
+I32 = mybir.dt.int32
+U32 = mybir.dt.uint32
+U8 = mybir.dt.uint8
+FP8 = mybir.dt.float8_e4m3fn
+FP8X4 = mybir.dt.float8_e4m3fn_x4
+FP4X4 = mybir.dt.float4_e2m1fn_x4
+ACT = mybir.ActivationFunctionType
+ALU = mybir.AluOpType
+
+SIZE = 1024
+P = 128
+HALF = 512
+FLOPS = 2 * 2 * SIZE * SIZE * SIZE
+
+
+def tile_lejepasigregrandomknotslicegrad_w4_kernel(tc, x_bytes, x_scale, w_words, w_scales, c, g, a_words, a_scales, s, out):
+    nc = tc.nc
+    with ExitStack() as ctx:
+        keep = ctx.enter_context(tc.tile_pool(name="keep", bufs=1))
+        work = ctx.enter_context(tc.tile_pool(name="work", bufs=2))
+        psum = ctx.enter_context(tc.psum_pool(name="psum", bufs=1))
+        ctx.enter_context(tc.manual_schedule())
+
+        ident = keep.tile([P, P], F32, name="ident")
+        warm = keep.tile([P, 8], F32, name="warm")
+        xs_all = keep.tile([P, SIZE], F32, name="xs_all")
+        w_raw = keep.tile([P, 2, 2048], U8, name="w_raw", align_bytes=64)
+        w_perm = keep.tile([P, 2, 2048], U8, name="w_perm", align_bytes=64)
+        ws_raw = keep.tile([P, 2, SIZE], U8, name="ws_raw", align_bytes=64)
+        ws_perm = keep.tile([P, 2, SIZE], U8, name="ws_perm", align_bytes=64)
+        a_raw = keep.tile([P, 2, 2048], U8, name="a_raw", align_bytes=64)
+        as_raw = keep.tile([P, 2, SIZE], U8, name="as_raw", align_bytes=64)
+        c_col = keep.tile([P, 2, 4], BF16, name="c_col")
+        g_col = keep.tile([P, 2, 4], BF16, name="g_col")
+        s_rows = keep.tile([8, P], BF16, name="s_rows")
+        s_rows32 = keep.tile([P, P], F32, name="s_rows32")
+        s_turns = keep.tile([P, 8], F32, name="s_turns")
+        s_pos = keep.tile([P, 8], F32, name="s_pos")
+        s_neg = keep.tile([P, 8], F32, name="s_neg")
+        s_sq = keep.tile([P, 8], F32, name="s_sq")
+        s_tanh = keep.tile([P, 8], F32, name="s_tanh")
+        psi_den = keep.tile([P, 8], F32, name="psi_den")
+        psi_rec = keep.tile([P, 8], F32, name="psi_rec")
+        psi_num = keep.tile([P, 8], F32, name="psi_num")
+        psi_sum = keep.tile([P, 8], F32, name="psi_sum")
+        sin_sum = keep.tile([P, 8], F32, name="sin_sum")
+        cos_sum = keep.tile([P, 8], F32, name="cos_sum")
+        x_tiles = [keep.tile([P, SIZE], U8, name="x_tile%d" % i) for i in range(8)]
+        x_grouped = [keep.tile([P, 2, HALF, 4], BF16, name="x_grouped%d" % h, align_bytes=64) for h in range(2)]
+        x_codes = [keep.tile([P, SIZE], U32, name="x_codes%d" % h, align_bytes=64) for h in range(2)]
+        x_planes = [keep.tile([P, SIZE], U8, name="x_planes%d" % h, align_bytes=64) for h in range(2)]
+        z_codes = [keep.tile([P, SIZE], U32, name="z_codes%d" % h, align_bytes=64) for h in range(2)]
+        z_planes = [keep.tile([P, SIZE], U8, name="z_planes%d" % h, align_bytes=64) for h in range(2)]
+
+        nc.vector.memset(ws_raw[:].rearrange("p g n -> p (g n)").bitcast(I32), 0)
+        nc.vector.memset(warm[:], 0.5)
+        nc.vector.memset(as_raw[:].rearrange("p g n -> p (g n)").bitcast(I32), 0)
+        nc.vector.memset(s_rows32[:], 0.0)
+        make_identity(nc, ident[:])
+        xs_row = x_scale.rearrange("o k -> (o k)")
+        nc.sync.dma_start(out=xs_all[:], in_=xs_row.partition_broadcast(P))
+        for i in range(2):
+            nc.sync.dma_start(out=x_tiles[i][:], in_=x_bytes[i * P:(i + 1) * P, :])
+        nc.sync.dma_start(out=w_raw[:].bitcast(I32), in_=w_words.rearrange("g p b -> p g b").bitcast(I32))
+        for q in range(4):
+            nc.scalar.dma_start(out=ws_raw[32 * q:32 * q + 4, :, :].bitcast(I32),
+                                in_=w_scales[:, 4 * q:4 * q + 4, :].rearrange("g r n -> r g n").bitcast(I32))
+        nc.scalar.activation(out=warm[:, 0:1], in_=warm[:, 1:2], func=ACT.Silu)
+        for i in range(2, 4):
+            nc.sync.dma_start(out=x_tiles[i][:], in_=x_bytes[i * P:(i + 1) * P, :])
+        nc.sync.dma_start(out=c_col[:], in_=c.rearrange("(G p t) -> p G t", p=P, t=4))
+        nc.sync.dma_start(out=g_col[:], in_=g.rearrange("(G p t) -> p G t", p=P, t=4))
+        nc.sync.dma_start(out=s_rows[:], in_=s.rearrange("(j p) -> j p", p=P))
+        for i in range(4, 8):
+            nc.sync.dma_start(out=x_tiles[i][:], in_=x_bytes[i * P:(i + 1) * P, :])
+        nc.sync.dma_start(out=a_raw[:].bitcast(I32), in_=a_words.rearrange("g p b -> p g b").bitcast(I32))
+        for q in range(4):
+            nc.sync.dma_start(out=as_raw[32 * q:32 * q + 4, :, :].bitcast(I32),
+                              in_=a_scales[:, 4 * q:4 * q + 4, :].rearrange("g r n -> r g n").bitcast(I32))
+
+        def widen_and_turn(i):
+            h, r = divmod(i, 4)
+            x_wide = work.tile([P, SIZE], BF16, name="x_wide", bufs=3)
+            nc.vector.tensor_tensor(out=x_wide[:], in0=x_tiles[i][:].bitcast(FP8), in1=xs_all[:], op=ALU.mult)
+            words = x_wide[:].bitcast(F32)
+            turned = psum.tile([P, 2, 2, P], F32, name="turned", bufs=4)
+            for k_pass in range(2):
+                for u in range(2):
+                    nc.tensor.transpose(turned[:, k_pass, u, :], words[:, 256 * k_pass + u:256 * (k_pass + 1):2], ident[:])
+            dst = x_grouped[h][:].rearrange("p g n t -> p g (n t)").bitcast(F32)
+            nc.scalar.copy(out=dst[:, :, 256 * r:256 * (r + 1)].rearrange("p g (n u) -> p g n u", u=2),
+                           in_=turned[:].rearrange("p g u n -> p g n u"))
+
+        def quantize_x(h):
+            nc.vector.quantize_mx(out=x_codes[h][:].bitcast(FP8X4), scales=x_planes[h][:],
+                                  in_=x_grouped[h][:].rearrange("p g n t -> p (g n t)"))
+
+        def permute_w(grp):
+            nc.vector.tensor_copy(
+                out=w_perm[:, :, 1024 * grp:1024 * (grp + 1)].rearrange("p g (t q b) -> p g t q b", t=4, b=2),
+                in_=w_raw[:, :, 1024 * grp:1024 * (grp + 1)].rearrange("p g (q t b) -> p g t q b", t=4, b=2))
+
+        def permute_w_scales():
+            nc.vector.tensor_copy(
+                out=ws_perm[:].rearrange("p g (G t q) -> p (g G) t q", G=2, t=4),
+                in_=ws_raw[:].rearrange("p g (G q t) -> p (g G) t q", G=2, t=4))
+
+        tanh_tiles = {}
+
+        def first_product(h, grp):
+            th = work.tile([P, 4, HALF], F32, name="th", bufs=3)
+            tanh_tiles[(h, grp)] = th
+            for t in range(4):
+                col = P * (4 * grp + t)
+                acc = psum.tile([P, HALF], F32, name="acc", bufs=4)
+                for k_pass in range(2):
+                    nc.tensor.matmul_mx(
+                        out=acc[:],
+                        lhsT=w_perm[:, k_pass, 2 * col:2 * (col + P)].bitcast(FP4X4),
+                        lhsT_scale=ws_perm[:, k_pass, col:col + P],
+                        rhs=x_codes[h][:, HALF * k_pass:HALF * (k_pass + 1)].bitcast(FP8X4),
+                        rhs_scale=x_planes[h][:, HALF * k_pass:HALF * (k_pass + 1)],
+                        start=(k_pass == 0), stop=(k_pass == 1))
+                nc.scalar.activation(out=th[:, t, :], in_=acc[:], func=ACT.Tanh, bias=c_col[:, grp, t:t + 1])
+
+        z_tiles = {}
+
+        def gain(h, grp):
+            z_grouped = work.tile([P, HALF, 4], BF16, name="z_grouped", bufs=2, align_bytes=64)
+            z_tiles[(h, grp)] = z_grouped
+            nc.vector.tensor_tensor(
+                out=z_grouped[:].rearrange("p (c i) t -> p c t i", i=4),
+                in0=tanh_tiles[(h, grp)][:].rearrange("p t (c i) -> p c t i", i=4),
+                in1=g_col[:, grp, :].unsqueeze(1).unsqueeze(3).to_broadcast([P, HALF // 4, 4, 4]),
+                op=ALU.mult)
+
+        def quantize_z(h, grp):
+            nc.vector.quantize_mx(out=z_codes[h][:, HALF * grp:HALF * (grp + 1)].bitcast(FP8X4),
+                                  scales=z_planes[h][:, HALF * grp:HALF * (grp + 1)],
+                                  in_=z_tiles[(h, grp)][:].rearrange("p n t -> p (n t)"))
+
+        banks, wholes, fracs = {}, {}, {}
+
+        def second_product(h, j):
+            acc = psum.tile([P, HALF], F32, name="acc", bufs=4)
+            banks[(h, j)] = acc
+            for grp in range(2):
+                nc.tensor.matmul_mx(
+                    out=acc[:],
+                    lhsT=a_raw[:, grp, 2 * P * j:2 * P * (j + 1)].bitcast(FP4X4),
+                    lhsT_scale=as_raw[:, grp, P * j:P * (j + 1)],
+                    rhs=z_codes[h][:, HALF * grp:HALF * (grp + 1)].bitcast(FP8X4),
+                    rhs_scale=z_planes[h][:, HALF * grp:HALF * (grp + 1)],
+                    start=(grp == 0), stop=(grp == 1))
+
+        def whole_turns(h, j):
+            whole = work.tile([P, HALF], I32, name="whole", bufs=3)
+            wholes[(h, j)] = whole
+            nc.vector.tensor_scalar(out=whole[:], in0=banks[(h, j)][:], scalar1=s_turns[:, j:j + 1], scalar2=None, op0=ALU.mult)
+
+        def fraction(h, j):
+            if h == 0:
+                fracs[j] = work.tile([P, SIZE], F32, name="frac", bufs=3)
+            nc.vector.scalar_tensor_tensor(out=fracs[j][:, HALF * h:HALF * (h + 1)], in0=banks[(h, j)][:], scalar=s_turns[:, j:j + 1],
+                                           in1=wholes[(h, j)][:], op0=ALU.mult, op1=ALU.subtract)
+
+        cos_u, sin_u = {}, {}
+
+        def trig(j):
+            frac = fracs[j]
+            size = work.tile([P, SIZE], F32, name="size", bufs=2)
+            cos_u[j] = work.tile([P, SIZE], F32, name="cos_u", bufs=4)
+            sin_u[j] = work.tile([P, SIZE], F32, name="sin_u", bufs=4)
+            nc.scalar.activation(out=size[:], in_=frac[:], func=ACT.Abs)
+            nc.scalar.activation(out=sin_u[j][:], in_=frac[:], func=ACT.Sin, scale=2.0 * math.pi,
+                                 accum_out=sin_sum[:, j:j + 1])
+            nc.scalar.activation(out=cos_u[j][:], in_=size[:], func=ACT.Sin, scale=-2.0 * math.pi,
+                                 bias=math.pi / 2.0, accum_out=cos_sum[:, j:j + 1])
+
+        factors = {}
+
+        def column_factors(j):
+            fac = work.tile([P, 1], F32, name="fac", bufs=3)
+            factors[j] = fac
+            nc.vector.tensor_tensor(out=fac[:], in0=cos_sum[:, j:j + 1], in1=psi_sum[:, j:j + 1], op=ALU.subtract)
+
+        def apply_factors(j, engine, cols):
+            engine.tensor_scalar(out=cos_u[j][:, cols], in0=cos_u[j][:, cols], scalar1=sin_sum[:, j:j + 1], scalar2=s_pos[:, j:j + 1],
+                                 op0=ALU.mult, op1=ALU.mult)
+            engine.tensor_scalar(out=sin_u[j][:, cols], in0=sin_u[j][:, cols], scalar1=factors[j][:], scalar2=s_neg[:, j:j + 1],
+                                 op0=ALU.mult, op1=ALU.mult)
+
+        out_banks = {}
+
+        def turn_back(j, h):
+            turned = psum.tile([P, 4, P], F32, name="turned", bufs=4)
+            out_banks[(j, h)] = turned
+            for r in range(4):
+                cols = slice(HALF * h + P * r, HALF * h + P * (r + 1))
+                nc.tensor.matmul(turned[:, r, :], lhsT=cos_u[j][:, cols], rhs=ident[:], is_transpose=True, start=True, stop=False)
+                nc.tensor.matmul(turned[:, r, :], lhsT=sin_u[j][:, cols], rhs=ident[:], is_transpose=True, start=False, stop=True)
+
+        out_view = out.rearrange("(h r p) m -> h p r m", h=2, p=P)
+
+        def store(j, h, on_vector):
+            staged = work.tile([P, 4, P], F32, name="staged", bufs=4)
+            if on_vector:
+                nc.vector.tensor_copy(out=staged[:], in_=out_banks[(j, h)][:])
+            else:
+                nc.scalar.copy(out=staged[:], in_=out_banks[(j, h)][:])
+            nc.sync.dma_start(out=out_view[h][:, :, P * j:P * (j + 1)], in_=staged[:])
+
+        def knots_turn():
+            nc.vector.tensor_copy(out=s_rows32[0:8, :], in_=s_rows[:])
+            turned = psum.tile([P, P], F32, name="turned", bufs=4)
+            nc.tensor.transpose(turned[:], s_rows32[:], ident[:])
+            nc.scalar.activation(out=s_sq[:], in_=turned[:, 0:8], func=ACT.Square)
+            nc.scalar.activation(out=s_turns[:], in_=turned[:, 0:8], func=ACT.Copy, scale=1.0 / (2.0 * math.pi))
+            nc.scalar.activation(out=s_pos[:], in_=turned[:, 0:8], func=ACT.Copy, scale=4.0 / SIZE)
+            nc.scalar.activation(out=s_neg[:], in_=turned[:, 0:8], func=ACT.Copy, scale=-4.0 / SIZE)
+            nc.scalar.activation(out=s_tanh[:], in_=s_sq[:], func=ACT.Tanh, scale=0.25)
+
+        widen_and_turn(0)
+        widen_and_turn(1)
+        permute_w(0)
+        widen_and_turn(2)
+        widen_and_turn(3)
+        permute_w_scales()
+        quantize_x(0)
+        permute_w(1)
+        knots_turn()
+        first_product(0, 0)
+        widen_and_turn(4)
+        widen_and_turn(5)
+        first_product(0, 1)
+        nc.vector.tensor_scalar(out=psi_den[:], in0=s_tanh[:], scalar1=1.0, scalar2=None, op0=ALU.add)
+        nc.vector.tensor_scalar(out=psi_num[:], in0=s_tanh[:], scalar1=-float(SIZE), scalar2=float(SIZE), op0=ALU.mult, op1=ALU.add)
+        widen_and_turn(6)
+        nc.vector.reciprocal(out=psi_rec[:], in_=psi_den[:])
+        widen_and_turn(7)
+        nc.vector.tensor_tensor(out=psi_sum[:], in0=psi_num[:], in1=psi_rec[:], op=ALU.mult)
+        gain(0, 0)
+        quantize_x(1)
+        quantize_z(0, 0)
+        first_product(1, 0)
+        gain(0, 1)
+        first_product(1, 1)
+        gain(1, 0)
+        quantize_z(0, 1)
+        second_product(0, 0)
+        gain(1, 1)
+        quantize_z(1, 0)
+        whole_turns(0, 0)
+        quantize_z(1, 1)
+        second_product(1, 0)
+        fraction(0, 0)
+        second_product(0, 1)
+        second_product(1, 1)
+        whole_turns(1, 0)
+        for j in range(8):
+            if j + 1 < 8:
+                whole_turns(0, j + 1)
+            fraction(1, j)
+            trig(j)
+            if j + 2 < 8:
+                second_product(0, j + 2)
+            if j + 1 < 8:
+                fraction(0, j + 1)
+            if j + 2 < 8:
+                second_product(1, j + 2)
+            if j >= 1:
+                column_factors(j - 1)
+                apply_factors(j - 1, nc.gpsimd, slice(0, SIZE))
+            if j + 1 < 8:
+                whole_turns(1, j + 1)
+            if j >= 3:
+                store(j - 3, 0, True)
+                store(j - 3, 1, True)
+            if j >= 2:
+                turn_back(j - 2, 0)
+                turn_back(j - 2, 1)
+        store(5, 0, True)
+        store(5, 1, True)
+        turn_back(6, 0)
+        turn_back(6, 1)
+        column_factors(7)
+        store(6, 0, True)
+        store(6, 1, True)
+        for h in range(2):
+            apply_factors(7, nc.vector, slice(HALF * h, HALF * (h + 1)))
+            turn_back(7, h)
+        store(7, 0, False)
+        store(7, 1, True)

@@ -18,6 +18,21 @@ ALU = mybir.AluOpType
 SIZE = 1024
 P = 128
 HALF = 512
+EARLY = 5
+LAG = 4
+RLAG = 2
+Z0 = 1
+Z1 = 3
+GLAST = 5
+TAILG = 4
+FRAC_BUFS = 6
+TRIG_BUFS = 8
+WARM0 = 0
+WARM1 = 0
+LEAD = 5
+TAILS = 2
+TAILV = 0
+ABS_ON_VECTOR = ()
 FLOPS = 2 * 2 * SIZE * SIZE * SIZE
 
 
@@ -31,9 +46,13 @@ def tile_lejepasigregrandomknotslicegrad_w4_kernel(tc, x_bytes, x_scale, w_words
 
         ident = keep.tile([P, P], F32, name="ident")
         warm = keep.tile([P, 8], F32, name="warm")
-        xs_all = keep.tile([P, SIZE], F32, name="xs_all")
-        w_raw = keep.tile([P, 2, 2048], U8, name="w_raw", align_bytes=64)
-        w_perm = keep.tile([P, 2, 2048], U8, name="w_perm", align_bytes=64)
+        xs_col = keep.tile([P, 2, 4], F32, name="xs_col")
+        w_raw = [keep.tile([P, 2, 1024], U8, name="w_raw%d" % grp, align_bytes=64) for grp in range(2)]
+        idle = keep.tile([P, HALF], BF16, name="idle")
+        early = keep.tile([P, 8, 2], F32, name="early")
+        late = keep.tile([P, 8, 2], F32, name="late")
+        rest = keep.tile([P, 8, 2], F32, name="rest")
+        w_perm = [keep.tile([P, 2, 1024], U8, name="w_perm%d" % grp, align_bytes=64) for grp in range(2)]
         ws_raw = keep.tile([P, 2, SIZE], U8, name="ws_raw", align_bytes=64)
         ws_perm = keep.tile([P, 2, SIZE], U8, name="ws_perm", align_bytes=64)
         a_raw = keep.tile([P, 2, 2048], U8, name="a_raw", align_bytes=64)
@@ -43,18 +62,15 @@ def tile_lejepasigregrandomknotslicegrad_w4_kernel(tc, x_bytes, x_scale, w_words
         s_rows = keep.tile([8, P], BF16, name="s_rows")
         s_rows32 = keep.tile([P, P], F32, name="s_rows32")
         s_turns = keep.tile([P, 8], F32, name="s_turns")
-        s_pos = keep.tile([P, 8], F32, name="s_pos")
-        s_neg = keep.tile([P, 8], F32, name="s_neg")
+        s_pair = keep.tile([P, 8, 2], F32, name="s_pair")
         s_sq = keep.tile([P, 8], F32, name="s_sq")
         s_tanh = keep.tile([P, 8], F32, name="s_tanh")
         psi_den = keep.tile([P, 8], F32, name="psi_den")
         psi_rec = keep.tile([P, 8], F32, name="psi_rec")
         psi_num = keep.tile([P, 8], F32, name="psi_num")
-        psi_sum = keep.tile([P, 8], F32, name="psi_sum")
-        sin_sum = keep.tile([P, 8], F32, name="sin_sum")
-        cos_sum = keep.tile([P, 8], F32, name="cos_sum")
         x_tiles = [keep.tile([P, SIZE], U8, name="x_tile%d" % i) for i in range(8)]
-        x_grouped = [keep.tile([P, 2, HALF, 4], BF16, name="x_grouped%d" % h, align_bytes=64) for h in range(2)]
+        x_wide = {}
+        x_grouped = [[keep.tile([P, HALF, 4], BF16, name="x_grouped%d_%d" % (h, k_pass), align_bytes=64) for k_pass in range(2)] for h in range(2)]
         x_codes = [keep.tile([P, SIZE], U32, name="x_codes%d" % h, align_bytes=64) for h in range(2)]
         x_planes = [keep.tile([P, SIZE], U8, name="x_planes%d" % h, align_bytes=64) for h in range(2)]
         z_codes = [keep.tile([P, SIZE], U32, name="z_codes%d" % h, align_bytes=64) for h in range(2)]
@@ -62,51 +78,83 @@ def tile_lejepasigregrandomknotslicegrad_w4_kernel(tc, x_bytes, x_scale, w_words
 
         nc.vector.memset(ws_raw[:].rearrange("p g n -> p (g n)").bitcast(I32), 0)
         nc.vector.memset(warm[:], 0.5)
+        nc.scalar.activation(out=warm[:, 0:1], in_=warm[:, 1:2], func=ACT.Silu)
+        make_identity(nc, ident[:])
         nc.vector.memset(as_raw[:].rearrange("p g n -> p (g n)").bitcast(I32), 0)
         nc.vector.memset(s_rows32[:], 0.0)
-        make_identity(nc, ident[:])
-        xs_row = x_scale.rearrange("o k -> (o k)")
-        nc.sync.dma_start(out=xs_all[:], in_=xs_row.partition_broadcast(P))
-        for i in range(2):
+        nc.vector.memset(rest[:], 0.0)
+
+        def keep_warm(count):
+            for repeat in range(count):
+                if repeat == 0:
+                    unused = psum.tile([P, HALF], F32, name="acc", bufs=4)
+                nc.tensor.matmul(unused[:], lhsT=idle[:, 0:P], rhs=idle[:], start=True, stop=True)
+
+        def load_w(grp):
+            nc.sync.dma_start(out=w_raw[grp][:].bitcast(I32),
+                              in_=w_words[:, :, 1024 * grp:1024 * (grp + 1)].rearrange("g p b -> p g b").bitcast(I32))
+
+        def load_x(i):
             nc.sync.dma_start(out=x_tiles[i][:], in_=x_bytes[i * P:(i + 1) * P, :])
-        nc.sync.dma_start(out=w_raw[:].bitcast(I32), in_=w_words.rearrange("g p b -> p g b").bitcast(I32))
+
+        load_w(0)
+        load_x(0)
+        load_x(1)
+        load_w(1)
         for q in range(4):
-            nc.scalar.dma_start(out=ws_raw[32 * q:32 * q + 4, :, :].bitcast(I32),
-                                in_=w_scales[:, 4 * q:4 * q + 4, :].rearrange("g r n -> r g n").bitcast(I32))
-        nc.scalar.activation(out=warm[:, 0:1], in_=warm[:, 1:2], func=ACT.Silu)
-        for i in range(2, 4):
-            nc.sync.dma_start(out=x_tiles[i][:], in_=x_bytes[i * P:(i + 1) * P, :])
+            nc.sync.dma_start(out=ws_raw[32 * q:32 * q + 4, :, :].bitcast(I32),
+                              in_=w_scales[:, 4 * q:4 * q + 4, :].rearrange("g r n -> r g n").bitcast(I32))
+        nc.sync.dma_start(out=xs_col[:], in_=x_scale.rearrange("o (g p t) -> p (o g) t", p=P, t=4))
+        load_x(2)
+        load_x(3)
+        load_x(4)
+        load_x(5)
         nc.sync.dma_start(out=c_col[:], in_=c.rearrange("(G p t) -> p G t", p=P, t=4))
-        nc.sync.dma_start(out=g_col[:], in_=g.rearrange("(G p t) -> p G t", p=P, t=4))
         nc.sync.dma_start(out=s_rows[:], in_=s.rearrange("(j p) -> j p", p=P))
-        for i in range(4, 8):
-            nc.sync.dma_start(out=x_tiles[i][:], in_=x_bytes[i * P:(i + 1) * P, :])
+        load_x(6)
+        load_x(7)
+        nc.sync.dma_start(out=g_col[:], in_=g.rearrange("(G p t) -> p G t", p=P, t=4))
         nc.sync.dma_start(out=a_raw[:].bitcast(I32), in_=a_words.rearrange("g p b -> p g b").bitcast(I32))
         for q in range(4):
             nc.sync.dma_start(out=as_raw[32 * q:32 * q + 4, :, :].bitcast(I32),
                               in_=a_scales[:, 4 * q:4 * q + 4, :].rearrange("g r n -> r g n").bitcast(I32))
 
-        def widen_and_turn(i):
-            h, r = divmod(i, 4)
-            x_wide = work.tile([P, SIZE], BF16, name="x_wide", bufs=3)
-            nc.vector.tensor_tensor(out=x_wide[:], in0=x_tiles[i][:].bitcast(FP8), in1=xs_all[:], op=ALU.mult)
-            words = x_wide[:].bitcast(F32)
-            turned = psum.tile([P, 2, 2, P], F32, name="turned", bufs=4)
-            for k_pass in range(2):
-                for u in range(2):
-                    nc.tensor.transpose(turned[:, k_pass, u, :], words[:, 256 * k_pass + u:256 * (k_pass + 1):2], ident[:])
-            dst = x_grouped[h][:].rearrange("p g n t -> p g (n t)").bitcast(F32)
-            nc.scalar.copy(out=dst[:, :, 256 * r:256 * (r + 1)].rearrange("p g (n u) -> p g n u", u=2),
-                           in_=turned[:].rearrange("p g u n -> p g n u"))
+        def widen(i, on_vector):
+            x_wide[i] = work.tile([P, SIZE], BF16, name="x_wide", bufs=6)
+            if on_vector:
+                nc.vector.tensor_copy(out=x_wide[i][:], in_=x_tiles[i][:].bitcast(FP8))
+            else:
+                nc.scalar.copy(out=x_wide[i][:], in_=x_tiles[i][:].bitcast(FP8))
 
-        def quantize_x(h):
-            nc.vector.quantize_mx(out=x_codes[h][:].bitcast(FP8X4), scales=x_planes[h][:],
-                                  in_=x_grouped[h][:].rearrange("p g n t -> p (g n t)"))
+        x_banks = {}
+
+        def turn(pair):
+            for k_pass in range(2):
+                x_banks[(pair, k_pass)] = psum.tile([P, 2, 2 * P], F32, name="turned", bufs=4)
+            for r in range(2):
+                words = x_wide[2 * pair + r][:].bitcast(F32)
+                for k_pass in range(2):
+                    for u in range(2):
+                        nc.tensor.transpose(x_banks[(pair, k_pass)][:, u, P * r:P * (r + 1)],
+                                            words[:, 256 * k_pass + u:256 * (k_pass + 1):2], ident[:])
+
+        def scale_x(pair, k_pass):
+            h, r = divmod(pair, 2)
+            nc.vector.tensor_tensor(
+                out=x_grouped[h][k_pass][:, 256 * r:256 * (r + 1), :].rearrange("p n (u e) -> p n u e", u=2),
+                in0=x_banks[(pair, k_pass)][:].bitcast(BF16).rearrange("p u (n e) -> p n u e", e=2),
+                in1=xs_col[:, k_pass, :].rearrange("p (u e) -> p u e", u=2).unsqueeze(1).to_broadcast([P, 256, 2, 2]),
+                op=ALU.mult)
+
+        def quantize_x(h, k_pass):
+            nc.vector.quantize_mx(out=x_codes[h][:, HALF * k_pass:HALF * (k_pass + 1)].bitcast(FP8X4),
+                                  scales=x_planes[h][:, HALF * k_pass:HALF * (k_pass + 1)],
+                                  in_=x_grouped[h][k_pass][:].rearrange("p n t -> p (n t)"))
 
         def permute_w(grp):
             nc.vector.tensor_copy(
-                out=w_perm[:, :, 1024 * grp:1024 * (grp + 1)].rearrange("p g (t q b) -> p g t q b", t=4, b=2),
-                in_=w_raw[:, :, 1024 * grp:1024 * (grp + 1)].rearrange("p g (q t b) -> p g t q b", t=4, b=2))
+                out=w_perm[grp][:].rearrange("p g (t q b) -> p g t q b", t=4, b=2),
+                in_=w_raw[grp][:].rearrange("p g (q t b) -> p g t q b", t=4, b=2))
 
         def permute_w_scales():
             nc.vector.tensor_copy(
@@ -124,7 +172,7 @@ def tile_lejepasigregrandomknotslicegrad_w4_kernel(tc, x_bytes, x_scale, w_words
                 for k_pass in range(2):
                     nc.tensor.matmul_mx(
                         out=acc[:],
-                        lhsT=w_perm[:, k_pass, 2 * col:2 * (col + P)].bitcast(FP4X4),
+                        lhsT=w_perm[grp][:, k_pass, 2 * P * t:2 * P * (t + 1)].bitcast(FP4X4),
                         lhsT_scale=ws_perm[:, k_pass, col:col + P],
                         rhs=x_codes[h][:, HALF * k_pass:HALF * (k_pass + 1)].bitcast(FP8X4),
                         rhs_scale=x_planes[h][:, HALF * k_pass:HALF * (k_pass + 1)],
@@ -168,45 +216,61 @@ def tile_lejepasigregrandomknotslicegrad_w4_kernel(tc, x_bytes, x_scale, w_words
 
         def fraction(h, j):
             if h == 0:
-                fracs[j] = work.tile([P, SIZE], F32, name="frac", bufs=3)
+                fracs[j] = work.tile([P, SIZE], F32, name="frac", bufs=FRAC_BUFS)
             nc.vector.scalar_tensor_tensor(out=fracs[j][:, HALF * h:HALF * (h + 1)], in0=banks[(h, j)][:], scalar=s_turns[:, j:j + 1],
                                            in1=wholes[(h, j)][:], op0=ALU.mult, op1=ALU.subtract)
 
         cos_u, sin_u = {}, {}
 
-        def trig(j):
+        def trig(j, cols, sums, between):
             frac = fracs[j]
             size = work.tile([P, SIZE], F32, name="size", bufs=2)
-            cos_u[j] = work.tile([P, SIZE], F32, name="cos_u", bufs=4)
-            sin_u[j] = work.tile([P, SIZE], F32, name="sin_u", bufs=4)
-            nc.scalar.activation(out=size[:], in_=frac[:], func=ACT.Abs)
-            nc.scalar.activation(out=sin_u[j][:], in_=frac[:], func=ACT.Sin, scale=2.0 * math.pi,
-                                 accum_out=sin_sum[:, j:j + 1])
-            nc.scalar.activation(out=cos_u[j][:], in_=size[:], func=ACT.Sin, scale=-2.0 * math.pi,
-                                 bias=math.pi / 2.0, accum_out=cos_sum[:, j:j + 1])
+            if j not in cos_u:
+                cos_u[j] = work.tile([P, SIZE], F32, name="cos_u", bufs=TRIG_BUFS)
+                sin_u[j] = work.tile([P, SIZE], F32, name="sin_u", bufs=TRIG_BUFS)
+            if j in ABS_ON_VECTOR:
+                nc.vector.scalar_tensor_tensor(out=size[:, cols], in0=frac[:, cols], scalar=-1.0, in1=frac[:, cols], op0=ALU.mult, op1=ALU.max)
+            else:
+                nc.scalar.activation(out=size[:, cols], in_=frac[:, cols], func=ACT.Abs)
+                between()
+            nc.scalar.activation(out=sin_u[j][:, cols], in_=frac[:, cols], func=ACT.Sin, scale=2.0 * math.pi,
+                                 accum_out=sums[:, j, 0:1])
+            if j in ABS_ON_VECTOR:
+                between()
+            nc.scalar.activation(out=cos_u[j][:, cols], in_=size[:, cols], func=ACT.Sin, scale=-2.0 * math.pi,
+                                 bias=math.pi / 2.0, accum_out=sums[:, j, 1:2])
 
-        factors = {}
+        totals = {}
 
-        def column_factors(j):
-            fac = work.tile([P, 1], F32, name="fac", bufs=3)
-            factors[j] = fac
-            nc.vector.tensor_tensor(out=fac[:], in0=cos_sum[:, j:j + 1], in1=psi_sum[:, j:j + 1], op=ALU.subtract)
+        def column_totals(j):
+            totals[j] = work.tile([P, 2], F32, name="totals", bufs=3)
+            for i in range(2):
+                nc.scalar.activation(out=totals[j][:, i:i + 1], in_=late[:, j, i:i + 1], func=ACT.Identity,
+                                     scale=s_pair[:, j, i:i + 1], bias=rest[:, j, i:i + 1])
 
-        def apply_factors(j, engine, cols):
-            engine.tensor_scalar(out=cos_u[j][:, cols], in0=cos_u[j][:, cols], scalar1=sin_sum[:, j:j + 1], scalar2=s_pos[:, j:j + 1],
-                                 op0=ALU.mult, op1=ALU.mult)
-            engine.tensor_scalar(out=sin_u[j][:, cols], in0=sin_u[j][:, cols], scalar1=factors[j][:], scalar2=s_neg[:, j:j + 1],
-                                 op0=ALU.mult, op1=ALU.mult)
+        def apply_factors(j):
+            nc.gpsimd.tensor_scalar(out=cos_u[j][:], in0=cos_u[j][:], scalar1=totals[j][:, 0:1], scalar2=0.0, op0=ALU.mult, op1=ALU.add)
+            nc.gpsimd.tensor_scalar(out=sin_u[j][:], in0=sin_u[j][:], scalar1=totals[j][:, 1:2], scalar2=0.0, op0=ALU.mult, op1=ALU.add)
+
+        def scale_cos(j, cols):
+            nc.vector.tensor_scalar(out=cos_u[j][:, cols], in0=cos_u[j][:, cols], scalar1=totals[j][:, 0:1], scalar2=None, op0=ALU.mult)
+
+        def combine(j, cols):
+            nc.vector.scalar_tensor_tensor(out=sin_u[j][:, cols], in0=sin_u[j][:, cols], scalar=totals[j][:, 1:2], in1=cos_u[j][:, cols],
+                                           op0=ALU.mult, op1=ALU.add)
 
         out_banks = {}
 
         def turn_back(j, h):
-            turned = psum.tile([P, 4, P], F32, name="turned", bufs=4)
+            turned = psum.tile([P, 4, P], F32, name="turned" if j < 6 else "acc", bufs=4)
             out_banks[(j, h)] = turned
             for r in range(4):
                 cols = slice(HALF * h + P * r, HALF * h + P * (r + 1))
-                nc.tensor.matmul(turned[:, r, :], lhsT=cos_u[j][:, cols], rhs=ident[:], is_transpose=True, start=True, stop=False)
-                nc.tensor.matmul(turned[:, r, :], lhsT=sin_u[j][:, cols], rhs=ident[:], is_transpose=True, start=False, stop=True)
+                if j < GLAST:
+                    nc.tensor.matmul(turned[:, r, :], lhsT=cos_u[j][:, cols], rhs=ident[:], is_transpose=True, start=True, stop=False)
+                    nc.tensor.matmul(turned[:, r, :], lhsT=sin_u[j][:, cols], rhs=ident[:], is_transpose=True, start=False, stop=True)
+                else:
+                    nc.tensor.transpose(turned[:, r, :], sin_u[j][:, cols], ident[:])
 
         out_view = out.rearrange("(h r p) m -> h p r m", h=2, p=P)
 
@@ -218,84 +282,150 @@ def tile_lejepasigregrandomknotslicegrad_w4_kernel(tc, x_bytes, x_scale, w_words
                 nc.scalar.copy(out=staged[:], in_=out_banks[(j, h)][:])
             nc.sync.dma_start(out=out_view[h][:, :, P * j:P * (j + 1)], in_=staged[:])
 
+        s_bank = psum.tile([P, P], F32, name="acc", bufs=4)
+
         def knots_turn():
             nc.vector.tensor_copy(out=s_rows32[0:8, :], in_=s_rows[:])
-            turned = psum.tile([P, P], F32, name="turned", bufs=4)
-            nc.tensor.transpose(turned[:], s_rows32[:], ident[:])
-            nc.scalar.activation(out=s_sq[:], in_=turned[:, 0:8], func=ACT.Square)
-            nc.scalar.activation(out=s_turns[:], in_=turned[:, 0:8], func=ACT.Copy, scale=1.0 / (2.0 * math.pi))
-            nc.scalar.activation(out=s_pos[:], in_=turned[:, 0:8], func=ACT.Copy, scale=4.0 / SIZE)
-            nc.scalar.activation(out=s_neg[:], in_=turned[:, 0:8], func=ACT.Copy, scale=-4.0 / SIZE)
-            nc.scalar.activation(out=s_tanh[:], in_=s_sq[:], func=ACT.Tanh, scale=0.25)
+            nc.tensor.transpose(s_bank[:], s_rows32[:], ident[:])
 
-        widen_and_turn(0)
-        widen_and_turn(1)
+        def knots_factors():
+            nc.scalar.activation(out=s_sq[:], in_=s_bank[:, 0:8], func=ACT.Square)
+            nc.scalar.activation(out=s_turns[:], in_=s_bank[:, 0:8], func=ACT.Copy, scale=1.0 / (2.0 * math.pi))
+            nc.scalar.activation(out=s_pair[:, :, 0], in_=s_bank[:, 0:8], func=ACT.Copy, scale=4.0 / SIZE)
+            nc.scalar.activation(out=s_pair[:, :, 1], in_=s_bank[:, 0:8], func=ACT.Copy, scale=-4.0 / SIZE)
+            nc.scalar.activation(out=s_tanh[:], in_=s_sq[:], func=ACT.Tanh, scale=0.25)
+            nc.scalar.activation(out=psi_den[:], in_=s_tanh[:], func=ACT.Identity, bias=1.0)
+            nc.scalar.activation(out=psi_num[:], in_=s_tanh[:], func=ACT.Identity, scale=float(SIZE), bias=-float(SIZE))
+
+        keep_warm(WARM0)
+        widen(0, False)
+        widen(1, False)
         permute_w(0)
-        widen_and_turn(2)
-        widen_and_turn(3)
-        permute_w_scales()
-        quantize_x(0)
+        turn(0)
+        widen(2, False)
+        widen(3, False)
         permute_w(1)
+        permute_w_scales()
+        turn(1)
+        scale_x(0, 0)
+        scale_x(0, 1)
+        widen(4, False)
+        widen(5, False)
         knots_turn()
+        turn(2)
+        scale_x(1, 0)
+        scale_x(1, 1)
+        widen(6, False)
+        widen(7, False)
+        knots_factors()
+        keep_warm(WARM1)
+        quantize_x(0, 0)
+        quantize_x(0, 1)
+        turn(3)
         first_product(0, 0)
-        widen_and_turn(4)
-        widen_and_turn(5)
+        scale_x(2, 0)
+        scale_x(2, 1)
         first_product(0, 1)
-        nc.vector.tensor_scalar(out=psi_den[:], in0=s_tanh[:], scalar1=1.0, scalar2=None, op0=ALU.add)
-        nc.vector.tensor_scalar(out=psi_num[:], in0=s_tanh[:], scalar1=-float(SIZE), scalar2=float(SIZE), op0=ALU.mult, op1=ALU.add)
-        widen_and_turn(6)
         nc.vector.reciprocal(out=psi_rec[:], in_=psi_den[:])
-        widen_and_turn(7)
-        nc.vector.tensor_tensor(out=psi_sum[:], in0=psi_num[:], in1=psi_rec[:], op=ALU.mult)
-        gain(0, 0)
-        quantize_x(1)
-        quantize_z(0, 0)
+        scale_x(3, 0)
+        scale_x(3, 1)
+        nc.vector.tensor_tensor(out=rest[:, :, 1], in0=psi_num[:], in1=psi_rec[:], op=ALU.mult)
+        quantize_x(1, 0)
+        quantize_x(1, 1)
         first_product(1, 0)
-        gain(0, 1)
+        gain(0, 0)
         first_product(1, 1)
-        gain(1, 0)
+        gain(0, 1)
+        quantize_z(0, 0)
         quantize_z(0, 1)
-        second_product(0, 0)
-        gain(1, 1)
-        quantize_z(1, 0)
-        whole_turns(0, 0)
-        quantize_z(1, 1)
-        second_product(1, 0)
-        fraction(0, 0)
-        second_product(0, 1)
-        second_product(1, 1)
-        whole_turns(1, 0)
+        units = [(0, j) for j in range(LEAD)]
         for j in range(8):
-            if j + 1 < 8:
-                whole_turns(0, j + 1)
-            fraction(1, j)
-            trig(j)
-            if j + 2 < 8:
-                second_product(0, j + 2)
-            if j + 1 < 8:
-                fraction(0, j + 1)
-            if j + 2 < 8:
-                second_product(1, j + 2)
-            if j >= 1:
-                column_factors(j - 1)
-                apply_factors(j - 1, nc.gpsimd, slice(0, SIZE))
-            if j + 1 < 8:
-                whole_turns(1, j + 1)
-            if j >= 3:
-                store(j - 3, 0, True)
-                store(j - 3, 1, True)
-            if j >= 2:
-                turn_back(j - 2, 0)
-                turn_back(j - 2, 1)
-        store(5, 0, True)
-        store(5, 1, True)
+            units.append((1, j))
+            if j + LEAD < 8:
+                units.append((0, j + LEAD))
+        second_half = {
+            Z0: [lambda: gain(1, 0)], Z0 + 1: [lambda: quantize_z(1, 0)],
+            Z1: [lambda: gain(1, 1)], Z1 + 1: [lambda: quantize_z(1, 1)]}
+        issued, done, ready, turned_halves, for_vector = [], [], [], [], []
+
+        def finish_sums(n):
+            for j in done:
+                column_totals(j)
+                if j < GLAST:
+                    apply_factors(j)
+                    ready.extend([(j, 0, n + LAG), (j, 1, n + LAG + 1)])
+                else:
+                    for_vector.append(j)
+            done.clear()
+
+        for unit in units[0:2]:
+            second_product(*unit)
+            issued.append(unit)
+        for n in range(len(units) + 1):
+            for unit in units[n:n + 2]:
+                if unit not in issued and (unit[0] == 0 or n > Z1 + 1):
+                    second_product(*unit)
+                    issued.append(unit)
+            if n < len(units):
+                whole_turns(*units[n])
+            if n == LEAD + 1:
+                nc.gpsimd.tensor_tensor(out=rest[:, 0:EARLY, :], in0=rest[:, 0:EARLY, :], in1=early[:, 0:EARLY, :], op=ALU.add)
+                nc.gpsimd.tensor_tensor(out=rest[:], in0=rest[:], in1=s_pair[:], op=ALU.mult)
+            if len(turned_halves) > 0 and turned_halves[0][2] <= n:
+                j, h, when = turned_halves.pop(0)
+                store(j, h, True)
+            if n >= 1:
+                h, j = units[n - 1]
+                fraction(h, j)
+                if h == 0 and j < EARLY:
+                    trig(j, slice(0, HALF), early, lambda: finish_sums(n))
+                if h == 1:
+                    trig(j, slice(HALF if j < EARLY else 0, SIZE), late, lambda: finish_sums(n))
+                    done.append(j)
+            for step in second_half.get(n, []):
+                step()
+            for unit in units[n + 2:n + 3]:
+                if unit[0] == 0 or n >= Z1 + 1:
+                    second_product(*unit)
+                    issued.append(unit)
+            if len(ready) > 0 and ready[0][2] <= n and len(turned_halves) < 3:
+                j, h, when = ready.pop(0)
+                turn_back(j, h)
+                turned_halves.append((j, h, n + 1))
+
+        def turn_and_store(j, h):
+            if len(turned_halves) == 2:
+                waiting = turned_halves.pop(0)
+                store(waiting[0], waiting[1], True)
+            turn_back(j, h)
+            turned_halves.append((j, h, 0))
+
+        for j, h, when in ready[0:TAILG]:
+            turn_and_store(j, h)
+        everything = slice(0, SIZE)
+        scale_cos(5, everything)
+        for j, h, when in ready[TAILG:]:
+            turn_and_store(j, h)
+        combine(5, everything)
+        for j, h, when in turned_halves[0:TAILS]:
+            store(j, h, True)
+        left = [(j, h) for j, h, when in turned_halves[TAILS:]]
+        scale_cos(6, everything)
+        turn_back(5, 0)
+        turn_back(5, 1)
+        combine(6, everything)
         turn_back(6, 0)
         turn_back(6, 1)
-        column_factors(7)
-        store(6, 0, True)
-        store(6, 1, True)
+        column_totals(7)
+        left = left + [(5, 0), (5, 1), (6, 0), (6, 1)]
+        for j, h in left[0:TAILV]:
+            store(j, h, True)
+        scale_cos(7, everything)
         for h in range(2):
-            apply_factors(7, nc.vector, slice(HALF * h, HALF * (h + 1)))
+            combine(7, slice(HALF * h, HALF * (h + 1)))
             turn_back(7, h)
-        store(7, 0, False)
-        store(7, 1, True)
+        for j, h in left[TAILV:-1]:
+            store(j, h, False)
+        store(6, 1, True)
+        store(7, 0, True)
+        store(7, 1, False)

@@ -17,23 +17,22 @@ ALU = mybir.AluOpType
 
 SIZE = 1024
 P = 128
+PACK = 4
 HALF = 512
-EARLY = 5
-LAG = 4
-RLAG = 2
-Z0 = 1
-Z1 = 3
-GLAST = 5
-TAILG = 4
-FRAC_BUFS = 6
-TRIG_BUFS = 8
-WARM0 = 0
-WARM1 = 0
-LEAD = 5
-TAILS = 2
-TAILV = 0
-ABS_ON_VECTOR = ()
+PAIR = 256
+GROUP = 512
+TILES = SIZE // P
+LAST_TILE = TILES - 1
+BANKS = 4
 FLOPS = 2 * 2 * SIZE * SIZE * SIZE
+
+EARLY_TILES = 4
+LEAD_TILES = EARLY_TILES + 1
+QUANTIZE_STEP = 3
+GPSIMD_TILES = 6
+TURN_STEP = 10
+HEAD_WARM_UPS = 7
+TAIL_WARM_UPS = 3
 
 
 def tile_lejepasigregrandomknotslicegrad_w4_kernel(tc, x_bytes, x_scale, w_words, w_scales, c, g, a_words, a_scales, s, out):
@@ -41,391 +40,361 @@ def tile_lejepasigregrandomknotslicegrad_w4_kernel(tc, x_bytes, x_scale, w_words
     with ExitStack() as ctx:
         keep = ctx.enter_context(tc.tile_pool(name="keep", bufs=1))
         work = ctx.enter_context(tc.tile_pool(name="work", bufs=2))
-        psum = ctx.enter_context(tc.psum_pool(name="psum", bufs=1))
+        psum = ctx.enter_context(tc.psum_pool(name="psum", bufs=BANKS))
         ctx.enter_context(tc.manual_schedule())
 
         ident = keep.tile([P, P], F32, name="ident")
-        warm = keep.tile([P, 8], F32, name="warm")
-        xs_col = keep.tile([P, 2, 4], F32, name="xs_col")
-        w_raw = [keep.tile([P, 2, 1024], U8, name="w_raw%d" % grp, align_bytes=64) for grp in range(2)]
-        idle = keep.tile([P, HALF], BF16, name="idle")
-        early = keep.tile([P, 8, 2], F32, name="early")
-        late = keep.tile([P, 8, 2], F32, name="late")
-        rest = keep.tile([P, 8, 2], F32, name="rest")
-        w_perm = [keep.tile([P, 2, 1024], U8, name="w_perm%d" % grp, align_bytes=64) for grp in range(2)]
-        ws_raw = keep.tile([P, 2, SIZE], U8, name="ws_raw", align_bytes=64)
-        ws_perm = keep.tile([P, 2, SIZE], U8, name="ws_perm", align_bytes=64)
-        a_raw = keep.tile([P, 2, 2048], U8, name="a_raw", align_bytes=64)
-        as_raw = keep.tile([P, 2, SIZE], U8, name="as_raw", align_bytes=64)
-        c_col = keep.tile([P, 2, 4], BF16, name="c_col")
-        g_col = keep.tile([P, 2, 4], BF16, name="g_col")
-        s_rows = keep.tile([8, P], BF16, name="s_rows")
-        s_rows32 = keep.tile([P, P], F32, name="s_rows32")
-        s_turns = keep.tile([P, 8], F32, name="s_turns")
-        s_pair = keep.tile([P, 8, 2], F32, name="s_pair")
-        s_sq = keep.tile([P, 8], F32, name="s_sq")
-        s_tanh = keep.tile([P, 8], F32, name="s_tanh")
-        psi_den = keep.tile([P, 8], F32, name="psi_den")
-        psi_rec = keep.tile([P, 8], F32, name="psi_rec")
-        psi_num = keep.tile([P, 8], F32, name="psi_num")
-        x_tiles = [keep.tile([P, SIZE], U8, name="x_tile%d" % i) for i in range(8)]
-        x_wide = {}
-        x_grouped = [[keep.tile([P, HALF, 4], BF16, name="x_grouped%d_%d" % (h, k_pass), align_bytes=64) for k_pass in range(2)] for h in range(2)]
-        x_codes = [keep.tile([P, SIZE], U32, name="x_codes%d" % h, align_bytes=64) for h in range(2)]
-        x_planes = [keep.tile([P, SIZE], U8, name="x_planes%d" % h, align_bytes=64) for h in range(2)]
-        z_codes = [keep.tile([P, SIZE], U32, name="z_codes%d" % h, align_bytes=64) for h in range(2)]
-        z_planes = [keep.tile([P, SIZE], U8, name="z_planes%d" % h, align_bytes=64) for h in range(2)]
+        table_probe = keep.tile([P, 2], F32, name="table_probe")
+        w_raw = [keep.tile([P, 2, 2 * GROUP], U8, name="w_raw%d" % grp, align_bytes=64) for grp in range(2)]
+        w_scales_raw = keep.tile([P, 2, SIZE], U8, name="w_scales_raw", align_bytes=64)
+        w_scales_sorted = keep.tile([P, 2, SIZE], U8, name="w_scales_sorted", align_bytes=64)
+        a_tile = keep.tile([P, 2, 2 * SIZE], U8, name="a_tile", align_bytes=64)
+        a_scales_tile = keep.tile([P, 2, SIZE], U8, name="a_scales_tile", align_bytes=64)
+        x_scale_col = keep.tile([P, 2, PACK], F32, name="x_scale_col")
+        c_col = keep.tile([P, 2, PACK], BF16, name="c_col")
+        g_col = keep.tile([P, 2, PACK], BF16, name="g_col")
+        s_rows = keep.tile([TILES, P], BF16, name="s_rows")
+        s_rows_padded = keep.tile([P, P], F32, name="s_rows_padded")
+        s_turns = keep.tile([P, TILES], F32, name="s_turns")
+        s_square = keep.tile([P, TILES], F32, name="s_square")
+        s_tanh = keep.tile([P, TILES], F32, name="s_tanh")
+        psi_denominator = keep.tile([P, TILES], F32, name="psi_denominator")
+        psi_reciprocal = keep.tile([P, TILES], F32, name="psi_reciprocal")
+        psi_numerator = keep.tile([P, TILES], F32, name="psi_numerator")
+        sum_gain = keep.tile([P, TILES, 2], F32, name="sum_gain")
+        early_sums = keep.tile([P, TILES, 2], F32, name="early_sums")
+        late_sums = keep.tile([P, TILES, 2], F32, name="late_sums")
+        factor_base = keep.tile([P, TILES, 2], F32, name="factor_base")
+        x_pairs = [keep.tile([P, 2, SIZE], U8, name="x_pair%d" % pair) for pair in range(4)]
+        x_grouped = [[keep.tile([P, HALF, PACK], BF16, name="x_grouped%d_%d" % (half, k_pass), align_bytes=64)
+                      for k_pass in range(2)] for half in range(2)]
+        x_codes = [keep.tile([P, SIZE], U32, name="x_codes%d" % half, align_bytes=64) for half in range(2)]
+        x_block_scales = [keep.tile([P, SIZE], U8, name="x_block_scales%d" % half, align_bytes=64) for half in range(2)]
+        z_codes = [keep.tile([P, SIZE], U32, name="z_codes%d" % half, align_bytes=64) for half in range(2)]
+        z_block_scales = [keep.tile([P, SIZE], U8, name="z_block_scales%d" % half, align_bytes=64) for half in range(2)]
 
-        nc.vector.memset(ws_raw[:].rearrange("p g n -> p (g n)").bitcast(I32), 0)
-        nc.vector.memset(warm[:], 0.5)
-        nc.scalar.activation(out=warm[:, 0:1], in_=warm[:, 1:2], func=ACT.Silu)
+        nc.vector.memset(w_scales_raw[:].rearrange("p g n -> p (g n)").bitcast(I32), 0)
+        nc.vector.memset(table_probe[:], 0.5)
+        nc.scalar.activation(out=table_probe[:, 0:1], in_=table_probe[:, 1:2], func=ACT.Silu)
         make_identity(nc, ident[:])
-        nc.vector.memset(as_raw[:].rearrange("p g n -> p (g n)").bitcast(I32), 0)
-        nc.vector.memset(s_rows32[:], 0.0)
-        nc.vector.memset(rest[:], 0.0)
+        nc.vector.memset(a_scales_tile[:].rearrange("p g n -> p (g n)").bitcast(I32), 0)
+        nc.vector.memset(s_rows_padded[:], 0.0)
+        nc.vector.memset(factor_base[:], 0.0)
 
-        def keep_warm(count):
+        def keep_tensor_warm(count):
+            unread = psum.tile([P, P], F32, name="product")
             for repeat in range(count):
-                if repeat == 0:
-                    unused = psum.tile([P, HALF], F32, name="acc", bufs=4)
-                nc.tensor.matmul(unused[:], lhsT=idle[:, 0:P], rhs=idle[:], start=True, stop=True)
+                nc.tensor.matmul(unread[:], lhsT=ident[:], rhs=ident[:], start=True, stop=True)
+
+        def load_x(pair):
+            src = x_bytes[PAIR * pair:PAIR * (pair + 1), :]
+            nc.sync.dma_start(out=x_pairs[pair][:], in_=src.rearrange("(r p) k -> p r k", p=P))
 
         def load_w(grp):
-            nc.sync.dma_start(out=w_raw[grp][:].bitcast(I32),
-                              in_=w_words[:, :, 1024 * grp:1024 * (grp + 1)].rearrange("g p b -> p g b").bitcast(I32))
+            src = w_words[:, :, 2 * GROUP * grp:2 * GROUP * (grp + 1)]
+            nc.sync.dma_start(out=w_raw[grp][:].bitcast(I32), in_=src.rearrange("g p b -> p g b").bitcast(I32))
 
-        def load_x(i):
-            nc.sync.dma_start(out=x_tiles[i][:], in_=x_bytes[i * P:(i + 1) * P, :])
+        def load_scale_rows(dst, scale_bytes):
+            for quadrant in range(4):
+                src = scale_bytes[:, 4 * quadrant:4 * quadrant + 4, :].rearrange("g r n -> r g n")
+                nc.sync.dma_start(out=dst[32 * quadrant:32 * quadrant + 4, :, :].bitcast(I32), in_=src.bitcast(I32))
 
-        load_w(0)
         load_x(0)
+        load_w(0)
         load_x(1)
+        nc.sync.dma_start(out=x_scale_col[:], in_=x_scale.rearrange("o (g p t) -> p (o g) t", p=P, t=PACK))
+        load_scale_rows(w_scales_raw, w_scales)
         load_w(1)
-        for q in range(4):
-            nc.sync.dma_start(out=ws_raw[32 * q:32 * q + 4, :, :].bitcast(I32),
-                              in_=w_scales[:, 4 * q:4 * q + 4, :].rearrange("g r n -> r g n").bitcast(I32))
-        nc.sync.dma_start(out=xs_col[:], in_=x_scale.rearrange("o (g p t) -> p (o g) t", p=P, t=4))
         load_x(2)
-        load_x(3)
-        load_x(4)
-        load_x(5)
-        nc.sync.dma_start(out=c_col[:], in_=c.rearrange("(G p t) -> p G t", p=P, t=4))
         nc.sync.dma_start(out=s_rows[:], in_=s.rearrange("(j p) -> j p", p=P))
-        load_x(6)
-        load_x(7)
-        nc.sync.dma_start(out=g_col[:], in_=g.rearrange("(G p t) -> p G t", p=P, t=4))
-        nc.sync.dma_start(out=a_raw[:].bitcast(I32), in_=a_words.rearrange("g p b -> p g b").bitcast(I32))
-        for q in range(4):
-            nc.sync.dma_start(out=as_raw[32 * q:32 * q + 4, :, :].bitcast(I32),
-                              in_=a_scales[:, 4 * q:4 * q + 4, :].rearrange("g r n -> r g n").bitcast(I32))
+        load_x(3)
+        nc.sync.dma_start(out=c_col[:], in_=c.rearrange("(G p t) -> p G t", p=P, t=PACK))
+        nc.sync.dma_start(out=g_col[:], in_=g.rearrange("(G p t) -> p G t", p=P, t=PACK))
+        nc.sync.dma_start(out=a_tile[:].bitcast(I32), in_=a_words.rearrange("g p b -> p g b").bitcast(I32))
+        load_scale_rows(a_scales_tile, a_scales)
 
-        def widen(i, on_vector):
-            x_wide[i] = work.tile([P, SIZE], BF16, name="x_wide", bufs=6)
-            if on_vector:
-                nc.vector.tensor_copy(out=x_wide[i][:], in_=x_tiles[i][:].bitcast(FP8))
-            else:
-                nc.scalar.copy(out=x_wide[i][:], in_=x_tiles[i][:].bitcast(FP8))
+        x_wide, x_banks = {}, {}
 
-        x_banks = {}
+        def widen_tile(pair, r):
+            x_wide[(pair, r)] = work.tile([P, SIZE], BF16, name="x_wide", bufs=6)
+            return x_wide[(pair, r)][:], x_pairs[pair][:, r, :].bitcast(FP8)
 
-        def turn(pair):
-            for k_pass in range(2):
-                x_banks[(pair, k_pass)] = psum.tile([P, 2, 2 * P], F32, name="turned", bufs=4)
+        def widen_pair_on_scalar(pair):
             for r in range(2):
-                words = x_wide[2 * pair + r][:].bitcast(F32)
+                wide, as_fp8 = widen_tile(pair, r)
+                nc.scalar.copy(out=wide, in_=as_fp8)
+
+        def turn_x(pair):
+            for k_pass in range(2):
+                x_banks[(pair, k_pass)] = psum.tile([P, 2, PAIR], F32, name="turned")
+            for r in range(2):
+                f_pairs = x_wide[(pair, r)][:].bitcast(F32)
                 for k_pass in range(2):
                     for u in range(2):
+                        first = GROUP // 2 * k_pass
                         nc.tensor.transpose(x_banks[(pair, k_pass)][:, u, P * r:P * (r + 1)],
-                                            words[:, 256 * k_pass + u:256 * (k_pass + 1):2], ident[:])
+                                            f_pairs[:, first + u:first + GROUP // 2:2], ident[:])
 
-        def scale_x(pair, k_pass):
-            h, r = divmod(pair, 2)
-            nc.vector.tensor_tensor(
-                out=x_grouped[h][k_pass][:, 256 * r:256 * (r + 1), :].rearrange("p n (u e) -> p n u e", u=2),
-                in0=x_banks[(pair, k_pass)][:].bitcast(BF16).rearrange("p u (n e) -> p n u e", e=2),
-                in1=xs_col[:, k_pass, :].rearrange("p (u e) -> p u e", u=2).unsqueeze(1).to_broadcast([P, 256, 2, 2]),
-                op=ALU.mult)
+        def scale_x(pair):
+            half, place = divmod(pair, 2)
+            for k_pass in range(2):
+                f_scale = x_scale_col[:, k_pass, :].rearrange("p (u e) -> p u e", u=2)
+                nc.vector.tensor_tensor(
+                    out=x_grouped[half][k_pass][:, PAIR * place:PAIR * (place + 1), :].rearrange("p n (u e) -> p n u e", u=2),
+                    in0=x_banks[(pair, k_pass)][:].bitcast(BF16).rearrange("p u (n e) -> p n u e", e=2),
+                    in1=f_scale.unsqueeze(1).to_broadcast([P, PAIR, 2, 2]),
+                    op=ALU.mult)
 
-        def quantize_x(h, k_pass):
-            nc.vector.quantize_mx(out=x_codes[h][:, HALF * k_pass:HALF * (k_pass + 1)].bitcast(FP8X4),
-                                  scales=x_planes[h][:, HALF * k_pass:HALF * (k_pass + 1)],
-                                  in_=x_grouped[h][k_pass][:].rearrange("p n t -> p (n t)"))
+        def quantize(codes, block_scales, k_pass, grouped):
+            cols = slice(HALF * k_pass, HALF * (k_pass + 1))
+            nc.vector.quantize_mx(out=codes[:, cols].bitcast(FP8X4), scales=block_scales[:, cols],
+                                  in_=grouped[:].rearrange("p n t -> p (n t)"))
 
-        def permute_w(grp):
-            nc.vector.tensor_copy(
-                out=w_perm[grp][:].rearrange("p g (t q b) -> p g t q b", t=4, b=2),
-                in_=w_raw[grp][:].rearrange("p g (q t b) -> p g t q b", t=4, b=2))
+        def quantize_x(half):
+            for k_pass in range(2):
+                quantize(x_codes[half], x_block_scales[half], k_pass, x_grouped[half][k_pass])
 
-        def permute_w_scales():
-            nc.vector.tensor_copy(
-                out=ws_perm[:].rearrange("p g (G t q) -> p (g G) t q", G=2, t=4),
-                in_=ws_raw[:].rearrange("p g (G q t) -> p (g G) t q", G=2, t=4))
+        w_sorted = {}
 
-        tanh_tiles = {}
+        def sort_first_w_group():
+            w_sorted[0] = keep.tile([P, 2, 2 * GROUP], U8, name="w_sorted0", align_bytes=64)
+            nc.vector.tensor_copy(out=w_sorted[0][:].rearrange("p g (t q b) -> p g t q b", t=PACK, b=2),
+                                  in_=w_raw[0][:].rearrange("p g (q t b) -> p g t q b", t=PACK, b=2))
 
-        def first_product(h, grp):
-            th = work.tile([P, 4, HALF], F32, name="th", bufs=3)
-            tanh_tiles[(h, grp)] = th
-            for t in range(4):
-                col = P * (4 * grp + t)
-                acc = psum.tile([P, HALF], F32, name="acc", bufs=4)
-                for k_pass in range(2):
-                    nc.tensor.matmul_mx(
-                        out=acc[:],
-                        lhsT=w_perm[grp][:, k_pass, 2 * P * t:2 * P * (t + 1)].bitcast(FP4X4),
-                        lhsT_scale=ws_perm[:, k_pass, col:col + P],
-                        rhs=x_codes[h][:, HALF * k_pass:HALF * (k_pass + 1)].bitcast(FP8X4),
-                        rhs_scale=x_planes[h][:, HALF * k_pass:HALF * (k_pass + 1)],
-                        start=(k_pass == 0), stop=(k_pass == 1))
-                nc.scalar.activation(out=th[:, t, :], in_=acc[:], func=ACT.Tanh, bias=c_col[:, grp, t:t + 1])
+        def sort_second_w_group():
+            w_sorted[1] = keep.tile([P, 2, 2 * GROUP], U8, name="w_sorted1", tag="x_grouped0_1", align_bytes=64)
+            for k_pass in range(2):
+                nc.gpsimd.tensor_copy(out=w_sorted[1][:, k_pass, :].rearrange("p (t q b) -> p t q b", t=PACK, b=2),
+                                      in_=w_raw[1][:, k_pass, :].rearrange("p (q t b) -> p t q b", t=PACK, b=2))
 
-        z_tiles = {}
+        def sort_w_scales():
+            nc.gpsimd.tensor_copy(out=w_scales_sorted[:].rearrange("p g (G t q) -> p (g G) t q", G=2, t=PACK),
+                                  in_=w_scales_raw[:].rearrange("p g (G q t) -> p (g G) t q", G=2, t=PACK))
 
-        def gain(h, grp):
-            z_grouped = work.tile([P, HALF, 4], BF16, name="z_grouped", bufs=2, align_bytes=64)
-            z_tiles[(h, grp)] = z_grouped
-            nc.vector.tensor_tensor(
-                out=z_grouped[:].rearrange("p (c i) t -> p c t i", i=4),
-                in0=tanh_tiles[(h, grp)][:].rearrange("p t (c i) -> p c t i", i=4),
-                in1=g_col[:, grp, :].unsqueeze(1).unsqueeze(3).to_broadcast([P, HALF // 4, 4, 4]),
-                op=ALU.mult)
-
-        def quantize_z(h, grp):
-            nc.vector.quantize_mx(out=z_codes[h][:, HALF * grp:HALF * (grp + 1)].bitcast(FP8X4),
-                                  scales=z_planes[h][:, HALF * grp:HALF * (grp + 1)],
-                                  in_=z_tiles[(h, grp)][:].rearrange("p n t -> p (n t)"))
-
-        banks, wholes, fracs = {}, {}, {}
-
-        def second_product(h, j):
-            acc = psum.tile([P, HALF], F32, name="acc", bufs=4)
-            banks[(h, j)] = acc
-            for grp in range(2):
+        def mx_product(words, word_col, scales, scale_col, codes, block_scales):
+            bank = psum.tile([P, HALF], F32, name="product")
+            for k_pass in range(2):
+                cols = slice(HALF * k_pass, HALF * (k_pass + 1))
                 nc.tensor.matmul_mx(
-                    out=acc[:],
-                    lhsT=a_raw[:, grp, 2 * P * j:2 * P * (j + 1)].bitcast(FP4X4),
-                    lhsT_scale=as_raw[:, grp, P * j:P * (j + 1)],
-                    rhs=z_codes[h][:, HALF * grp:HALF * (grp + 1)].bitcast(FP8X4),
-                    rhs_scale=z_planes[h][:, HALF * grp:HALF * (grp + 1)],
-                    start=(grp == 0), stop=(grp == 1))
+                    out=bank[:],
+                    lhsT=words[:, k_pass, 2 * word_col:2 * (word_col + P)].bitcast(FP4X4),
+                    lhsT_scale=scales[:, k_pass, scale_col:scale_col + P],
+                    rhs=codes[:, cols].bitcast(FP8X4), rhs_scale=block_scales[:, cols],
+                    start=(k_pass == 0), stop=(k_pass == 1))
+            return bank
 
-        def whole_turns(h, j):
-            whole = work.tile([P, HALF], I32, name="whole", bufs=3)
-            wholes[(h, j)] = whole
-            nc.vector.tensor_scalar(out=whole[:], in0=banks[(h, j)][:], scalar1=s_turns[:, j:j + 1], scalar2=None, op0=ALU.mult)
+        tanh_tiles, z_grouped = {}, {}
 
-        def fraction(h, j):
-            if h == 0:
-                fracs[j] = work.tile([P, SIZE], F32, name="frac", bufs=FRAC_BUFS)
-            nc.vector.scalar_tensor_tensor(out=fracs[j][:, HALF * h:HALF * (h + 1)], in0=banks[(h, j)][:], scalar=s_turns[:, j:j + 1],
-                                           in1=wholes[(h, j)][:], op0=ALU.mult, op1=ALU.subtract)
+        def first_product(half, grp):
+            tanh_tiles[(half, grp)] = work.tile([P, PACK, HALF], F32, name="tanh_tile", bufs=3)
+            for t in range(PACK):
+                bank = mx_product(w_sorted[grp], P * t, w_scales_sorted, GROUP * grp + P * t, x_codes[half], x_block_scales[half])
+                nc.scalar.activation(out=tanh_tiles[(half, grp)][:, t, :], in_=bank[:], func=ACT.Tanh, bias=c_col[:, grp, t:t + 1])
 
-        cos_u, sin_u = {}, {}
+        def z_tile(half, grp):
+            z_grouped[(half, grp)] = work.tile([P, HALF, PACK], BF16, name="z_grouped", bufs=3, align_bytes=64)
+            return z_grouped[(half, grp)]
 
-        def trig(j, cols, sums, between):
-            frac = fracs[j]
-            size = work.tile([P, SIZE], F32, name="size", bufs=2)
-            if j not in cos_u:
-                cos_u[j] = work.tile([P, SIZE], F32, name="cos_u", bufs=TRIG_BUFS)
-                sin_u[j] = work.tile([P, SIZE], F32, name="sin_u", bufs=TRIG_BUFS)
-            if j in ABS_ON_VECTOR:
-                nc.vector.scalar_tensor_tensor(out=size[:, cols], in0=frac[:, cols], scalar=-1.0, in1=frac[:, cols], op0=ALU.mult, op1=ALU.max)
+        def gain_on_vector(half, grp):
+            nc.vector.tensor_tensor(
+                out=z_tile(half, grp)[:].rearrange("p (n i) t -> p n t i", i=4),
+                in0=tanh_tiles[(half, grp)][:].rearrange("p t (n i) -> p n t i", i=4),
+                in1=g_col[:, grp, :].unsqueeze(1).unsqueeze(3).to_broadcast([P, HALF // 4, PACK, 4]),
+                op=ALU.mult)
+
+        def gain_on_gpsimd(half, grp):
+            nc.gpsimd.tensor_tensor(
+                out=z_tile(half, grp)[:], in0=tanh_tiles[(half, grp)][:].rearrange("p t n -> p n t"),
+                in1=g_col[:, grp, :].unsqueeze(1).to_broadcast([P, HALF, PACK]), op=ALU.mult)
+
+        def quantize_z(half):
+            for grp in range(2):
+                quantize(z_codes[half], z_block_scales[half], grp, z_grouped[(half, grp)])
+
+        def turn_s():
+            nc.scalar.copy(out=s_rows_padded[0:TILES, :], in_=s_rows[:])
+            bank = psum.tile([P, P], F32, name="product")
+            nc.tensor.transpose(bank[:], s_rows_padded[:], ident[:])
+            return bank[:, 0:TILES]
+
+        def factors_of_s(s_col):
+            nc.scalar.activation(out=s_square[:], in_=s_col, func=ACT.Square)
+            nc.scalar.activation(out=s_turns[:], in_=s_col, func=ACT.Copy, scale=1.0 / (2.0 * math.pi))
+            nc.scalar.activation(out=sum_gain[:, :, 0], in_=s_col, func=ACT.Copy, scale=4.0 / SIZE)
+            nc.scalar.activation(out=sum_gain[:, :, 1], in_=s_col, func=ACT.Copy, scale=-4.0 / SIZE)
+            nc.scalar.activation(out=s_tanh[:], in_=s_square[:], func=ACT.Tanh, scale=0.25)
+            nc.scalar.activation(out=psi_denominator[:], in_=s_tanh[:], func=ACT.Identity, bias=1.0)
+            nc.scalar.activation(out=psi_numerator[:], in_=s_tanh[:], func=ACT.Identity, scale=float(SIZE), bias=-float(SIZE))
+
+        unit_banks, wholes, fracs, cos_u, sin_u, factors, out_banks = {}, {}, {}, {}, {}, {}, {}
+        all_rows = slice(0, SIZE)
+
+        def half_rows(half):
+            return slice(HALF * half, HALF * (half + 1))
+
+        def second_product(half, j):
+            unit_banks[(half, j)] = mx_product(a_tile, P * j, a_scales_tile, P * j, z_codes[half], z_block_scales[half])
+
+        def whole_turns(half, j):
+            wholes[(half, j)] = work.tile([P, HALF], I32, name="whole", bufs=3)
+            nc.vector.tensor_scalar(out=wholes[(half, j)][:], in0=unit_banks[(half, j)][:], scalar1=s_turns[:, j:j + 1],
+                                    scalar2=None, op0=ALU.mult)
+
+        def fraction(half, j):
+            if half == 0:
+                fracs[j] = work.tile([P, SIZE], F32, name="frac", bufs=LEAD_TILES + 1)
+            nc.vector.scalar_tensor_tensor(out=fracs[j][:, half_rows(half)], in0=unit_banks[(half, j)][:], scalar=s_turns[:, j:j + 1],
+                                           in1=wholes[(half, j)][:], op0=ALU.mult, op1=ALU.subtract)
+
+        def magnitude(j, rows):
+            size = work.tile([P, SIZE], F32, name="size")
+            if j == LAST_TILE:
+                nc.vector.tensor_reduce(out=size[:, rows], in_=fracs[j][:, rows].unsqueeze(2), axis=mybir.AxisListType.X,
+                                        op=ALU.max, apply_absolute_value=True, opt_input=False)
             else:
-                nc.scalar.activation(out=size[:, cols], in_=frac[:, cols], func=ACT.Abs)
-                between()
-            nc.scalar.activation(out=sin_u[j][:, cols], in_=frac[:, cols], func=ACT.Sin, scale=2.0 * math.pi,
+                nc.scalar.activation(out=size[:, rows], in_=fracs[j][:, rows], func=ACT.Abs)
+            return size
+
+        def sin_and_cos(j, rows, size, sums):
+            if j not in sin_u:
+                cos_u[j] = keep.tile([P, SIZE], F32, name="cos_u%d" % j)
+                sin_u[j] = keep.tile([P, SIZE], F32, name="sin_u%d" % j)
+            nc.scalar.activation(out=sin_u[j][:, rows], in_=fracs[j][:, rows], func=ACT.Sin, scale=2.0 * math.pi,
                                  accum_out=sums[:, j, 0:1])
-            if j in ABS_ON_VECTOR:
-                between()
-            nc.scalar.activation(out=cos_u[j][:, cols], in_=size[:, cols], func=ACT.Sin, scale=-2.0 * math.pi,
+            nc.scalar.activation(out=cos_u[j][:, rows], in_=size[:, rows], func=ACT.Sin, scale=-2.0 * math.pi,
                                  bias=math.pi / 2.0, accum_out=sums[:, j, 1:2])
 
-        totals = {}
+        def fold_early_sums():
+            early = slice(0, EARLY_TILES)
+            nc.gpsimd.tensor_tensor(out=factor_base[:, early, :], in0=factor_base[:, early, :], in1=early_sums[:, early, :], op=ALU.add)
+            nc.gpsimd.tensor_tensor(out=factor_base[:], in0=factor_base[:], in1=sum_gain[:], op=ALU.mult)
 
-        def column_totals(j):
-            totals[j] = work.tile([P, 2], F32, name="totals", bufs=3)
+        def scale_on_gpsimd(j):
+            factors[j] = work.tile([P, 2], F32, name="factors", bufs=3)
             for i in range(2):
-                nc.scalar.activation(out=totals[j][:, i:i + 1], in_=late[:, j, i:i + 1], func=ACT.Identity,
-                                     scale=s_pair[:, j, i:i + 1], bias=rest[:, j, i:i + 1])
+                nc.scalar.activation(out=factors[j][:, i:i + 1], in_=late_sums[:, j, i:i + 1], func=ACT.Identity,
+                                     scale=sum_gain[:, j, i:i + 1], bias=factor_base[:, j, i:i + 1])
+            for i, term in enumerate((cos_u[j], sin_u[j])):
+                nc.gpsimd.tensor_scalar(out=term[:], in0=term[:], scalar1=factors[j][:, i:i + 1], scalar2=0.0,
+                                        op0=ALU.mult, op1=ALU.add)
 
-        def apply_factors(j):
-            nc.gpsimd.tensor_scalar(out=cos_u[j][:], in0=cos_u[j][:], scalar1=totals[j][:, 0:1], scalar2=0.0, op0=ALU.mult, op1=ALU.add)
-            nc.gpsimd.tensor_scalar(out=sin_u[j][:], in0=sin_u[j][:], scalar1=totals[j][:, 1:2], scalar2=0.0, op0=ALU.mult, op1=ALU.add)
+        def scale_cos_on_vector(j):
+            factors[j] = work.tile([P, 2], F32, name="factors", bufs=3)
+            nc.vector.tensor_scalar(out=factors[j][:, 1:2], in0=late_sums[:, j, 1:2], scalar1=sum_gain[:, j, 1:2],
+                                    scalar2=factor_base[:, j, 1:2], op0=ALU.mult, op1=ALU.add)
+            nc.vector.tensor_scalar(out=cos_u[j][:], in0=cos_u[j][:], scalar1=late_sums[:, j, 0:1], scalar2=sum_gain[:, j, 0:1],
+                                    op0=ALU.mult, op1=ALU.mult)
 
-        def scale_cos(j, cols):
-            nc.vector.tensor_scalar(out=cos_u[j][:, cols], in0=cos_u[j][:, cols], scalar1=totals[j][:, 0:1], scalar2=None, op0=ALU.mult)
+        def combine_on_vector(j, half):
+            rows = half_rows(half)
+            nc.vector.scalar_tensor_tensor(out=sin_u[j][:, rows], in0=sin_u[j][:, rows], scalar=factors[j][:, 1:2],
+                                           in1=cos_u[j][:, rows], op0=ALU.mult, op1=ALU.add)
 
-        def combine(j, cols):
-            nc.vector.scalar_tensor_tensor(out=sin_u[j][:, cols], in0=sin_u[j][:, cols], scalar=totals[j][:, 1:2], in1=cos_u[j][:, cols],
-                                           op0=ALU.mult, op1=ALU.add)
-
-        out_banks = {}
-
-        def turn_back(j, h):
-            turned = psum.tile([P, 4, P], F32, name="turned" if j < 6 else "acc", bufs=4)
-            out_banks[(j, h)] = turned
+        def turn_back_and_add(j, half):
+            out_banks[(j, half)] = psum.tile([P, 4, P], F32, name="turned")
             for r in range(4):
-                cols = slice(HALF * h + P * r, HALF * h + P * (r + 1))
-                if j < GLAST:
-                    nc.tensor.matmul(turned[:, r, :], lhsT=cos_u[j][:, cols], rhs=ident[:], is_transpose=True, start=True, stop=False)
-                    nc.tensor.matmul(turned[:, r, :], lhsT=sin_u[j][:, cols], rhs=ident[:], is_transpose=True, start=False, stop=True)
-                else:
-                    nc.tensor.transpose(turned[:, r, :], sin_u[j][:, cols], ident[:])
+                rows = slice(HALF * half + P * r, HALF * half + P * (r + 1))
+                for i, term in enumerate((cos_u[j], sin_u[j])):
+                    nc.tensor.matmul(out_banks[(j, half)][:, r, :], lhsT=term[:, rows], rhs=ident[:], is_transpose=True,
+                                     start=(i == 0), stop=(i == 1))
+            if half == 1 and 0 < j < GPSIMD_TILES - 1:
+                keep_tensor_warm(TAIL_WARM_UPS)
 
-        out_view = out.rearrange("(h r p) m -> h p r m", h=2, p=P)
+        def turn_back(j, half):
+            out_banks[(j, half)] = psum.tile([P, 4, P], F32, name="product")
+            for r in range(4):
+                rows = slice(HALF * half + P * r, HALF * half + P * (r + 1))
+                nc.tensor.transpose(out_banks[(j, half)][:, r, :], sin_u[j][:, rows], ident[:])
 
-        def store(j, h, on_vector):
-            staged = work.tile([P, 4, P], F32, name="staged", bufs=4)
+        out_rows = out.rearrange("(h r p) m -> h p r m", h=2, p=P)
+
+        def store(j, half, on_vector):
+            staged = work.tile([P, 4, P], F32, name="staged", bufs=BANKS)
             if on_vector:
-                nc.vector.tensor_copy(out=staged[:], in_=out_banks[(j, h)][:])
+                nc.vector.tensor_copy(out=staged[:], in_=out_banks[(j, half)][:])
             else:
-                nc.scalar.copy(out=staged[:], in_=out_banks[(j, h)][:])
-            nc.sync.dma_start(out=out_view[h][:, :, P * j:P * (j + 1)], in_=staged[:])
+                nc.scalar.copy(out=staged[:], in_=out_banks[(j, half)][:])
+            nc.sync.dma_start(out=out_rows[half][:, :, P * j:P * (j + 1)], in_=staged[:])
 
-        s_bank = psum.tile([P, P], F32, name="acc", bufs=4)
-
-        def knots_turn():
-            nc.vector.tensor_copy(out=s_rows32[0:8, :], in_=s_rows[:])
-            nc.tensor.transpose(s_bank[:], s_rows32[:], ident[:])
-
-        def knots_factors():
-            nc.scalar.activation(out=s_sq[:], in_=s_bank[:, 0:8], func=ACT.Square)
-            nc.scalar.activation(out=s_turns[:], in_=s_bank[:, 0:8], func=ACT.Copy, scale=1.0 / (2.0 * math.pi))
-            nc.scalar.activation(out=s_pair[:, :, 0], in_=s_bank[:, 0:8], func=ACT.Copy, scale=4.0 / SIZE)
-            nc.scalar.activation(out=s_pair[:, :, 1], in_=s_bank[:, 0:8], func=ACT.Copy, scale=-4.0 / SIZE)
-            nc.scalar.activation(out=s_tanh[:], in_=s_sq[:], func=ACT.Tanh, scale=0.25)
-            nc.scalar.activation(out=psi_den[:], in_=s_tanh[:], func=ACT.Identity, bias=1.0)
-            nc.scalar.activation(out=psi_num[:], in_=s_tanh[:], func=ACT.Identity, scale=float(SIZE), bias=-float(SIZE))
-
-        keep_warm(WARM0)
-        widen(0, False)
-        widen(1, False)
-        permute_w(0)
-        turn(0)
-        widen(2, False)
-        widen(3, False)
-        permute_w(1)
-        permute_w_scales()
-        turn(1)
-        scale_x(0, 0)
-        scale_x(0, 1)
-        widen(4, False)
-        widen(5, False)
-        knots_turn()
-        turn(2)
-        scale_x(1, 0)
-        scale_x(1, 1)
-        widen(6, False)
-        widen(7, False)
-        knots_factors()
-        keep_warm(WARM1)
-        quantize_x(0, 0)
-        quantize_x(0, 1)
-        turn(3)
+        keep_tensor_warm(HEAD_WARM_UPS)
+        wide, as_fp8 = widen_tile(0, 0)
+        nc.vector.tensor_copy(out=wide, in_=as_fp8)
+        wide, as_fp8 = widen_tile(0, 1)
+        nc.scalar.copy(out=wide, in_=as_fp8)
+        sort_first_w_group()
+        turn_x(0)
+        widen_pair_on_scalar(1)
+        sort_w_scales()
+        turn_x(1)
+        scale_x(0)
+        widen_pair_on_scalar(2)
+        turn_x(2)
+        s_col = turn_s()
+        scale_x(1)
+        widen_pair_on_scalar(3)
+        factors_of_s(s_col)
+        quantize_x(0)
+        sort_second_w_group()
+        turn_x(3)
         first_product(0, 0)
-        scale_x(2, 0)
-        scale_x(2, 1)
+        scale_x(2)
         first_product(0, 1)
-        nc.vector.reciprocal(out=psi_rec[:], in_=psi_den[:])
-        scale_x(3, 0)
-        scale_x(3, 1)
-        nc.vector.tensor_tensor(out=rest[:, :, 1], in0=psi_num[:], in1=psi_rec[:], op=ALU.mult)
-        quantize_x(1, 0)
-        quantize_x(1, 1)
+        scale_x(3)
+        nc.vector.reciprocal(out=psi_reciprocal[:], in_=psi_denominator[:])
+        quantize_x(1)
+        nc.vector.tensor_tensor(out=factor_base[:, :, 1], in0=psi_numerator[:], in1=psi_reciprocal[:], op=ALU.mult)
         first_product(1, 0)
-        gain(0, 0)
+        gain_on_vector(0, 0)
         first_product(1, 1)
-        gain(0, 1)
-        quantize_z(0, 0)
-        quantize_z(0, 1)
-        units = [(0, j) for j in range(LEAD)]
-        for j in range(8):
-            units.append((1, j))
-            if j + LEAD < 8:
-                units.append((0, j + LEAD))
-        second_half = {
-            Z0: [lambda: gain(1, 0)], Z0 + 1: [lambda: quantize_z(1, 0)],
-            Z1: [lambda: gain(1, 1)], Z1 + 1: [lambda: quantize_z(1, 1)]}
-        issued, done, ready, turned_halves, for_vector = [], [], [], [], []
+        gain_on_vector(0, 1)
+        quantize_z(0)
 
-        def finish_sums(n):
-            for j in done:
-                column_totals(j)
-                if j < GLAST:
-                    apply_factors(j)
-                    ready.extend([(j, 0, n + LAG), (j, 1, n + LAG + 1)])
-                else:
-                    for_vector.append(j)
-            done.clear()
+        units = [(half, j) for half in range(2) for j in range(LEAD_TILES)]
+        units.extend([(half, j) for j in range(LEAD_TILES, TILES) for half in range(2)])
+        gpsimd_halves = [(j, half) for j in range(GPSIMD_TILES) for half in range(2)]
 
-        for unit in units[0:2]:
-            second_product(*unit)
-            issued.append(unit)
-        for n in range(len(units) + 1):
-            for unit in units[n:n + 2]:
-                if unit not in issued and (unit[0] == 0 or n > Z1 + 1):
-                    second_product(*unit)
-                    issued.append(unit)
-            if n < len(units):
-                whole_turns(*units[n])
-            if n == LEAD + 1:
-                nc.gpsimd.tensor_tensor(out=rest[:, 0:EARLY, :], in0=rest[:, 0:EARLY, :], in1=early[:, 0:EARLY, :], op=ALU.add)
-                nc.gpsimd.tensor_tensor(out=rest[:], in0=rest[:], in1=s_pair[:], op=ALU.mult)
-            if len(turned_halves) > 0 and turned_halves[0][2] <= n:
-                j, h, when = turned_halves.pop(0)
-                store(j, h, True)
-            if n >= 1:
-                h, j = units[n - 1]
-                fraction(h, j)
-                if h == 0 and j < EARLY:
-                    trig(j, slice(0, HALF), early, lambda: finish_sums(n))
-                if h == 1:
-                    trig(j, slice(HALF if j < EARLY else 0, SIZE), late, lambda: finish_sums(n))
-                    done.append(j)
-            for step in second_half.get(n, []):
-                step()
-            for unit in units[n + 2:n + 3]:
-                if unit[0] == 0 or n >= Z1 + 1:
-                    second_product(*unit)
-                    issued.append(unit)
-            if len(ready) > 0 and ready[0][2] <= n and len(turned_halves) < 3:
-                j, h, when = ready.pop(0)
-                turn_back(j, h)
-                turned_halves.append((j, h, n + 1))
+        second_product(*units[0])
+        second_product(*units[1])
+        gain_on_vector(1, 0)
+        gain_on_gpsimd(1, 1)
+        for step in range(len(units) + 1):
+            if step < len(units):
+                whole_turns(*units[step])
+            if step == LEAD_TILES + 1:
+                fold_early_sums()
+            if step > TURN_STEP:
+                store(*gpsimd_halves[step - TURN_STEP - 1], on_vector=True)
+            if step > 0:
+                half, j = units[step - 1]
+                fraction(half, j)
+                if half == 0 and j < EARLY_TILES:
+                    sin_and_cos(j, half_rows(0), magnitude(j, half_rows(0)), early_sums)
+                if half == 1:
+                    rows = half_rows(1) if j < EARLY_TILES else all_rows
+                    size = magnitude(j, rows)
+                    if 1 < j <= GPSIMD_TILES:
+                        scale_on_gpsimd(j - 1)
+                    sin_and_cos(j, rows, size, late_sums)
+                    if j == 0:
+                        scale_on_gpsimd(0)
+            if step == QUANTIZE_STEP:
+                quantize_z(1)
+            if step + 2 < len(units):
+                second_product(*units[step + 2])
+            if step >= TURN_STEP:
+                turn_back_and_add(*gpsimd_halves[step - TURN_STEP])
 
-        def turn_and_store(j, h):
-            if len(turned_halves) == 2:
-                waiting = turned_halves.pop(0)
-                store(waiting[0], waiting[1], True)
-            turn_back(j, h)
-            turned_halves.append((j, h, 0))
-
-        for j, h, when in ready[0:TAILG]:
-            turn_and_store(j, h)
-        everything = slice(0, SIZE)
-        scale_cos(5, everything)
-        for j, h, when in ready[TAILG:]:
-            turn_and_store(j, h)
-        combine(5, everything)
-        for j, h, when in turned_halves[0:TAILS]:
-            store(j, h, True)
-        left = [(j, h) for j, h, when in turned_halves[TAILS:]]
-        scale_cos(6, everything)
-        turn_back(5, 0)
-        turn_back(5, 1)
-        combine(6, everything)
-        turn_back(6, 0)
-        turn_back(6, 1)
-        column_totals(7)
-        left = left + [(5, 0), (5, 1), (6, 0), (6, 1)]
-        for j, h in left[0:TAILV]:
-            store(j, h, True)
-        scale_cos(7, everything)
-        for h in range(2):
-            combine(7, slice(HALF * h, HALF * (h + 1)))
-            turn_back(7, h)
-        for j, h in left[TAILV:-1]:
-            store(j, h, False)
-        store(6, 1, True)
-        store(7, 0, True)
-        store(7, 1, False)
+        turned_so_far = len(units) + 1 - TURN_STEP
+        for i in range(turned_so_far, len(gpsimd_halves) + 1):
+            j, half = gpsimd_halves[i - 1]
+            if i < len(gpsimd_halves):
+                turn_back_and_add(*gpsimd_halves[i])
+            store(j, half, on_vector=(j < GPSIMD_TILES - 1))
+        for j in range(GPSIMD_TILES, TILES):
+            scale_cos_on_vector(j)
+            for half in range(2):
+                combine_on_vector(j, half)
+                turn_back(j, half)
+        for j in range(GPSIMD_TILES, TILES):
+            for half in range(2):
+                store(j, half, on_vector=(j == LAST_TILE and half == 0))

from contextlib import ExitStack
import math

import concourse.mybir as mybir
from concourse.masks import make_identity

F32 = mybir.dt.float32
BF16 = mybir.dt.bfloat16
I32 = mybir.dt.int32
U32 = mybir.dt.uint32
U8 = mybir.dt.uint8
FP8 = mybir.dt.float8_e4m3fn
FP8X4 = mybir.dt.float8_e4m3fn_x4
FP4X4 = mybir.dt.float4_e2m1fn_x4
ACT = mybir.ActivationFunctionType
ALU = mybir.AluOpType

SIZE = 1024
P = 128
PACK = 4
HALF = 512
PAIR = 256
GROUP = 512
TILES = SIZE // P
LAST_TILE = TILES - 1
BANKS = 4
FLOPS = 2 * 2 * SIZE * SIZE * SIZE

EARLY_TILES = 4
LEAD_TILES = EARLY_TILES + 1
QUANTIZE_STEP = 3
GPSIMD_TILES = 6
TURN_STEP = 10
HEAD_WARM_UPS = 7
TAIL_WARM_UPS = 3


def tile_lejepasigregrandomknotslicegrad_w4_kernel(tc, x_bytes, x_scale, w_words, w_scales, c, g, a_words, a_scales, s, out):
    nc = tc.nc
    with ExitStack() as ctx:
        keep = ctx.enter_context(tc.tile_pool(name="keep", bufs=1))
        work = ctx.enter_context(tc.tile_pool(name="work", bufs=2))
        psum = ctx.enter_context(tc.psum_pool(name="psum", bufs=BANKS))
        ctx.enter_context(tc.manual_schedule())

        ident = keep.tile([P, P], F32, name="ident")
        table_probe = keep.tile([P, 2], F32, name="table_probe")
        w_raw = [keep.tile([P, 2, 2 * GROUP], U8, name="w_raw%d" % grp, align_bytes=64) for grp in range(2)]
        w_scales_raw = keep.tile([P, 2, SIZE], U8, name="w_scales_raw", align_bytes=64)
        w_scales_sorted = keep.tile([P, 2, SIZE], U8, name="w_scales_sorted", align_bytes=64)
        a_tile = keep.tile([P, 2, 2 * SIZE], U8, name="a_tile", align_bytes=64)
        a_scales_tile = keep.tile([P, 2, SIZE], U8, name="a_scales_tile", align_bytes=64)
        x_scale_col = keep.tile([P, 2, PACK], F32, name="x_scale_col")
        c_col = keep.tile([P, 2, PACK], BF16, name="c_col")
        g_col = keep.tile([P, 2, PACK], BF16, name="g_col")
        s_rows = keep.tile([TILES, P], BF16, name="s_rows")
        s_rows_padded = keep.tile([P, P], F32, name="s_rows_padded")
        s_turns = keep.tile([P, TILES], F32, name="s_turns")
        s_square = keep.tile([P, TILES], F32, name="s_square")
        s_tanh = keep.tile([P, TILES], F32, name="s_tanh")
        psi_denominator = keep.tile([P, TILES], F32, name="psi_denominator")
        psi_reciprocal = keep.tile([P, TILES], F32, name="psi_reciprocal")
        psi_numerator = keep.tile([P, TILES], F32, name="psi_numerator")
        sum_gain = keep.tile([P, TILES, 2], F32, name="sum_gain")
        early_sums = keep.tile([P, TILES, 2], F32, name="early_sums")
        late_sums = keep.tile([P, TILES, 2], F32, name="late_sums")
        factor_base = keep.tile([P, TILES, 2], F32, name="factor_base")
        x_pairs = [keep.tile([P, 2, SIZE], U8, name="x_pair%d" % pair) for pair in range(4)]
        x_grouped = [[keep.tile([P, HALF, PACK], BF16, name="x_grouped%d_%d" % (half, k_pass), align_bytes=64)
                      for k_pass in range(2)] for half in range(2)]
        x_codes = [keep.tile([P, SIZE], U32, name="x_codes%d" % half, align_bytes=64) for half in range(2)]
        x_block_scales = [keep.tile([P, SIZE], U8, name="x_block_scales%d" % half, align_bytes=64) for half in range(2)]
        z_codes = [keep.tile([P, SIZE], U32, name="z_codes%d" % half, align_bytes=64) for half in range(2)]
        z_block_scales = [keep.tile([P, SIZE], U8, name="z_block_scales%d" % half, align_bytes=64) for half in range(2)]

        nc.vector.memset(w_scales_raw[:].rearrange("p g n -> p (g n)").bitcast(I32), 0)
        nc.vector.memset(table_probe[:], 0.5)
        nc.scalar.activation(out=table_probe[:, 0:1], in_=table_probe[:, 1:2], func=ACT.Silu)
        make_identity(nc, ident[:])
        nc.vector.memset(a_scales_tile[:].rearrange("p g n -> p (g n)").bitcast(I32), 0)
        nc.vector.memset(s_rows_padded[:], 0.0)
        nc.vector.memset(factor_base[:], 0.0)

        def keep_tensor_warm(count):
            unread = psum.tile([P, P], F32, name="product")
            for repeat in range(count):
                nc.tensor.matmul(unread[:], lhsT=ident[:], rhs=ident[:], start=True, stop=True)

        def load_x(pair):
            src = x_bytes[PAIR * pair:PAIR * (pair + 1), :]
            nc.sync.dma_start(out=x_pairs[pair][:], in_=src.rearrange("(r p) k -> p r k", p=P))

        def load_w(grp):
            src = w_words[:, :, 2 * GROUP * grp:2 * GROUP * (grp + 1)]
            nc.sync.dma_start(out=w_raw[grp][:].bitcast(I32), in_=src.rearrange("g p b -> p g b").bitcast(I32))

        def load_scale_rows(dst, scale_bytes):
            for quadrant in range(4):
                src = scale_bytes[:, 4 * quadrant:4 * quadrant + 4, :].rearrange("g r n -> r g n")
                nc.sync.dma_start(out=dst[32 * quadrant:32 * quadrant + 4, :, :].bitcast(I32), in_=src.bitcast(I32))

        load_x(0)
        load_w(0)
        load_x(1)
        nc.sync.dma_start(out=x_scale_col[:], in_=x_scale.rearrange("o (g p t) -> p (o g) t", p=P, t=PACK))
        load_scale_rows(w_scales_raw, w_scales)
        load_w(1)
        load_x(2)
        nc.sync.dma_start(out=s_rows[:], in_=s.rearrange("(j p) -> j p", p=P))
        load_x(3)
        nc.sync.dma_start(out=c_col[:], in_=c.rearrange("(G p t) -> p G t", p=P, t=PACK))
        nc.sync.dma_start(out=g_col[:], in_=g.rearrange("(G p t) -> p G t", p=P, t=PACK))
        nc.sync.dma_start(out=a_tile[:].bitcast(I32), in_=a_words.rearrange("g p b -> p g b").bitcast(I32))
        load_scale_rows(a_scales_tile, a_scales)

        x_wide, x_banks = {}, {}

        def widen_tile(pair, r):
            x_wide[(pair, r)] = work.tile([P, SIZE], BF16, name="x_wide", bufs=6)
            return x_wide[(pair, r)][:], x_pairs[pair][:, r, :].bitcast(FP8)

        def widen_pair_on_scalar(pair):
            for r in range(2):
                wide, as_fp8 = widen_tile(pair, r)
                nc.scalar.copy(out=wide, in_=as_fp8)

        def turn_x(pair):
            for k_pass in range(2):
                x_banks[(pair, k_pass)] = psum.tile([P, 2, PAIR], F32, name="turned")
            for r in range(2):
                f_pairs = x_wide[(pair, r)][:].bitcast(F32)
                for k_pass in range(2):
                    for u in range(2):
                        first = GROUP // 2 * k_pass
                        nc.tensor.transpose(x_banks[(pair, k_pass)][:, u, P * r:P * (r + 1)],
                                            f_pairs[:, first + u:first + GROUP // 2:2], ident[:])

        def scale_x(pair):
            half, place = divmod(pair, 2)
            for k_pass in range(2):
                f_scale = x_scale_col[:, k_pass, :].rearrange("p (u e) -> p u e", u=2)
                nc.vector.tensor_tensor(
                    out=x_grouped[half][k_pass][:, PAIR * place:PAIR * (place + 1), :].rearrange("p n (u e) -> p n u e", u=2),
                    in0=x_banks[(pair, k_pass)][:].bitcast(BF16).rearrange("p u (n e) -> p n u e", e=2),
                    in1=f_scale.unsqueeze(1).to_broadcast([P, PAIR, 2, 2]),
                    op=ALU.mult)

        def quantize(codes, block_scales, k_pass, grouped):
            cols = slice(HALF * k_pass, HALF * (k_pass + 1))
            nc.vector.quantize_mx(out=codes[:, cols].bitcast(FP8X4), scales=block_scales[:, cols],
                                  in_=grouped[:].rearrange("p n t -> p (n t)"))

        def quantize_x(half):
            for k_pass in range(2):
                quantize(x_codes[half], x_block_scales[half], k_pass, x_grouped[half][k_pass])

        w_sorted = {}

        def sort_first_w_group():
            w_sorted[0] = keep.tile([P, 2, 2 * GROUP], U8, name="w_sorted0", align_bytes=64)
            nc.vector.tensor_copy(out=w_sorted[0][:].rearrange("p g (t q b) -> p g t q b", t=PACK, b=2),
                                  in_=w_raw[0][:].rearrange("p g (q t b) -> p g t q b", t=PACK, b=2))

        def sort_second_w_group():
            w_sorted[1] = keep.tile([P, 2, 2 * GROUP], U8, name="w_sorted1", tag="x_grouped0_1", align_bytes=64)
            for k_pass in range(2):
                nc.gpsimd.tensor_copy(out=w_sorted[1][:, k_pass, :].rearrange("p (t q b) -> p t q b", t=PACK, b=2),
                                      in_=w_raw[1][:, k_pass, :].rearrange("p (q t b) -> p t q b", t=PACK, b=2))

        def sort_w_scales():
            nc.gpsimd.tensor_copy(out=w_scales_sorted[:].rearrange("p g (G t q) -> p (g G) t q", G=2, t=PACK),
                                  in_=w_scales_raw[:].rearrange("p g (G q t) -> p (g G) t q", G=2, t=PACK))

        def mx_product(words, word_col, scales, scale_col, codes, block_scales):
            bank = psum.tile([P, HALF], F32, name="product")
            for k_pass in range(2):
                cols = slice(HALF * k_pass, HALF * (k_pass + 1))
                nc.tensor.matmul_mx(
                    out=bank[:],
                    lhsT=words[:, k_pass, 2 * word_col:2 * (word_col + P)].bitcast(FP4X4),
                    lhsT_scale=scales[:, k_pass, scale_col:scale_col + P],
                    rhs=codes[:, cols].bitcast(FP8X4), rhs_scale=block_scales[:, cols],
                    start=(k_pass == 0), stop=(k_pass == 1))
            return bank

        tanh_tiles, z_grouped = {}, {}

        def first_product(half, grp):
            tanh_tiles[(half, grp)] = work.tile([P, PACK, HALF], F32, name="tanh_tile", bufs=3)
            for t in range(PACK):
                bank = mx_product(w_sorted[grp], P * t, w_scales_sorted, GROUP * grp + P * t, x_codes[half], x_block_scales[half])
                nc.scalar.activation(out=tanh_tiles[(half, grp)][:, t, :], in_=bank[:], func=ACT.Tanh, bias=c_col[:, grp, t:t + 1])

        def z_tile(half, grp):
            z_grouped[(half, grp)] = work.tile([P, HALF, PACK], BF16, name="z_grouped", bufs=3, align_bytes=64)
            return z_grouped[(half, grp)]

        def gain_on_vector(half, grp):
            nc.vector.tensor_tensor(
                out=z_tile(half, grp)[:].rearrange("p (n i) t -> p n t i", i=4),
                in0=tanh_tiles[(half, grp)][:].rearrange("p t (n i) -> p n t i", i=4),
                in1=g_col[:, grp, :].unsqueeze(1).unsqueeze(3).to_broadcast([P, HALF // 4, PACK, 4]),
                op=ALU.mult)

        def gain_on_gpsimd(half, grp):
            nc.gpsimd.tensor_tensor(
                out=z_tile(half, grp)[:], in0=tanh_tiles[(half, grp)][:].rearrange("p t n -> p n t"),
                in1=g_col[:, grp, :].unsqueeze(1).to_broadcast([P, HALF, PACK]), op=ALU.mult)

        def quantize_z(half):
            for grp in range(2):
                quantize(z_codes[half], z_block_scales[half], grp, z_grouped[(half, grp)])

        def turn_s():
            nc.scalar.copy(out=s_rows_padded[0:TILES, :], in_=s_rows[:])
            bank = psum.tile([P, P], F32, name="product")
            nc.tensor.transpose(bank[:], s_rows_padded[:], ident[:])
            return bank[:, 0:TILES]

        def factors_of_s(s_col):
            nc.scalar.activation(out=s_square[:], in_=s_col, func=ACT.Square)
            nc.scalar.activation(out=s_turns[:], in_=s_col, func=ACT.Copy, scale=1.0 / (2.0 * math.pi))
            nc.scalar.activation(out=sum_gain[:, :, 0], in_=s_col, func=ACT.Copy, scale=4.0 / SIZE)
            nc.scalar.activation(out=sum_gain[:, :, 1], in_=s_col, func=ACT.Copy, scale=-4.0 / SIZE)
            nc.scalar.activation(out=s_tanh[:], in_=s_square[:], func=ACT.Tanh, scale=0.25)
            nc.scalar.activation(out=psi_denominator[:], in_=s_tanh[:], func=ACT.Identity, bias=1.0)
            nc.scalar.activation(out=psi_numerator[:], in_=s_tanh[:], func=ACT.Identity, scale=float(SIZE), bias=-float(SIZE))

        unit_banks, wholes, fracs, cos_u, sin_u, factors, out_banks = {}, {}, {}, {}, {}, {}, {}
        all_rows = slice(0, SIZE)

        def half_rows(half):
            return slice(HALF * half, HALF * (half + 1))

        def second_product(half, j):
            unit_banks[(half, j)] = mx_product(a_tile, P * j, a_scales_tile, P * j, z_codes[half], z_block_scales[half])

        def whole_turns(half, j):
            wholes[(half, j)] = work.tile([P, HALF], I32, name="whole", bufs=3)
            nc.vector.tensor_scalar(out=wholes[(half, j)][:], in0=unit_banks[(half, j)][:], scalar1=s_turns[:, j:j + 1],
                                    scalar2=None, op0=ALU.mult)

        def fraction(half, j):
            if half == 0:
                fracs[j] = work.tile([P, SIZE], F32, name="frac", bufs=LEAD_TILES + 1)
            nc.vector.scalar_tensor_tensor(out=fracs[j][:, half_rows(half)], in0=unit_banks[(half, j)][:], scalar=s_turns[:, j:j + 1],
                                           in1=wholes[(half, j)][:], op0=ALU.mult, op1=ALU.subtract)

        def magnitude(j, rows):
            size = work.tile([P, SIZE], F32, name="size")
            if j == LAST_TILE:
                nc.vector.tensor_reduce(out=size[:, rows], in_=fracs[j][:, rows].unsqueeze(2), axis=mybir.AxisListType.X,
                                        op=ALU.max, apply_absolute_value=True, opt_input=False)
            else:
                nc.scalar.activation(out=size[:, rows], in_=fracs[j][:, rows], func=ACT.Abs)
            return size

        def sin_and_cos(j, rows, size, sums):
            if j not in sin_u:
                cos_u[j] = keep.tile([P, SIZE], F32, name="cos_u%d" % j)
                sin_u[j] = keep.tile([P, SIZE], F32, name="sin_u%d" % j)
            nc.scalar.activation(out=sin_u[j][:, rows], in_=fracs[j][:, rows], func=ACT.Sin, scale=2.0 * math.pi,
                                 accum_out=sums[:, j, 0:1])
            nc.scalar.activation(out=cos_u[j][:, rows], in_=size[:, rows], func=ACT.Sin, scale=-2.0 * math.pi,
                                 bias=math.pi / 2.0, accum_out=sums[:, j, 1:2])

        def fold_early_sums():
            early = slice(0, EARLY_TILES)
            nc.gpsimd.tensor_tensor(out=factor_base[:, early, :], in0=factor_base[:, early, :], in1=early_sums[:, early, :], op=ALU.add)
            nc.gpsimd.tensor_tensor(out=factor_base[:], in0=factor_base[:], in1=sum_gain[:], op=ALU.mult)

        def scale_on_gpsimd(j):
            factors[j] = work.tile([P, 2], F32, name="factors", bufs=3)
            for i in range(2):
                nc.scalar.activation(out=factors[j][:, i:i + 1], in_=late_sums[:, j, i:i + 1], func=ACT.Identity,
                                     scale=sum_gain[:, j, i:i + 1], bias=factor_base[:, j, i:i + 1])
            for i, term in enumerate((cos_u[j], sin_u[j])):
                nc.gpsimd.tensor_scalar(out=term[:], in0=term[:], scalar1=factors[j][:, i:i + 1], scalar2=0.0,
                                        op0=ALU.mult, op1=ALU.add)

        def scale_cos_on_vector(j):
            factors[j] = work.tile([P, 2], F32, name="factors", bufs=3)
            nc.vector.tensor_scalar(out=factors[j][:, 1:2], in0=late_sums[:, j, 1:2], scalar1=sum_gain[:, j, 1:2],
                                    scalar2=factor_base[:, j, 1:2], op0=ALU.mult, op1=ALU.add)
            nc.vector.tensor_scalar(out=cos_u[j][:], in0=cos_u[j][:], scalar1=late_sums[:, j, 0:1], scalar2=sum_gain[:, j, 0:1],
                                    op0=ALU.mult, op1=ALU.mult)

        def combine_on_vector(j, half):
            rows = half_rows(half)
            nc.vector.scalar_tensor_tensor(out=sin_u[j][:, rows], in0=sin_u[j][:, rows], scalar=factors[j][:, 1:2],
                                           in1=cos_u[j][:, rows], op0=ALU.mult, op1=ALU.add)

        def turn_back_and_add(j, half):
            out_banks[(j, half)] = psum.tile([P, 4, P], F32, name="turned")
            for r in range(4):
                rows = slice(HALF * half + P * r, HALF * half + P * (r + 1))
                for i, term in enumerate((cos_u[j], sin_u[j])):
                    nc.tensor.matmul(out_banks[(j, half)][:, r, :], lhsT=term[:, rows], rhs=ident[:], is_transpose=True,
                                     start=(i == 0), stop=(i == 1))
            if half == 1 and 0 < j < GPSIMD_TILES - 1:
                keep_tensor_warm(TAIL_WARM_UPS)

        def turn_back(j, half):
            out_banks[(j, half)] = psum.tile([P, 4, P], F32, name="product")
            for r in range(4):
                rows = slice(HALF * half + P * r, HALF * half + P * (r + 1))
                nc.tensor.transpose(out_banks[(j, half)][:, r, :], sin_u[j][:, rows], ident[:])

        out_rows = out.rearrange("(h r p) m -> h p r m", h=2, p=P)

        def store(j, half, on_vector):
            staged = work.tile([P, 4, P], F32, name="staged", bufs=BANKS)
            if on_vector:
                nc.vector.tensor_copy(out=staged[:], in_=out_banks[(j, half)][:])
            else:
                nc.scalar.copy(out=staged[:], in_=out_banks[(j, half)][:])
            nc.sync.dma_start(out=out_rows[half][:, :, P * j:P * (j + 1)], in_=staged[:])

        keep_tensor_warm(HEAD_WARM_UPS)
        wide, as_fp8 = widen_tile(0, 0)
        nc.vector.tensor_copy(out=wide, in_=as_fp8)
        wide, as_fp8 = widen_tile(0, 1)
        nc.scalar.copy(out=wide, in_=as_fp8)
        sort_first_w_group()
        turn_x(0)
        widen_pair_on_scalar(1)
        sort_w_scales()
        turn_x(1)
        scale_x(0)
        widen_pair_on_scalar(2)
        turn_x(2)
        s_col = turn_s()
        scale_x(1)
        widen_pair_on_scalar(3)
        factors_of_s(s_col)
        quantize_x(0)
        sort_second_w_group()
        turn_x(3)
        first_product(0, 0)
        scale_x(2)
        first_product(0, 1)
        scale_x(3)
        nc.vector.reciprocal(out=psi_reciprocal[:], in_=psi_denominator[:])
        quantize_x(1)
        nc.vector.tensor_tensor(out=factor_base[:, :, 1], in0=psi_numerator[:], in1=psi_reciprocal[:], op=ALU.mult)
        first_product(1, 0)
        gain_on_vector(0, 0)
        first_product(1, 1)
        gain_on_vector(0, 1)
        quantize_z(0)

        units = [(half, j) for half in range(2) for j in range(LEAD_TILES)]
        units.extend([(half, j) for j in range(LEAD_TILES, TILES) for half in range(2)])
        gpsimd_halves = [(j, half) for j in range(GPSIMD_TILES) for half in range(2)]

        second_product(*units[0])
        second_product(*units[1])
        gain_on_vector(1, 0)
        gain_on_gpsimd(1, 1)
        for step in range(len(units) + 1):
            if step < len(units):
                whole_turns(*units[step])
            if step == LEAD_TILES + 1:
                fold_early_sums()
            if step > TURN_STEP:
                store(*gpsimd_halves[step - TURN_STEP - 1], on_vector=True)
            if step > 0:
                half, j = units[step - 1]
                fraction(half, j)
                if half == 0 and j < EARLY_TILES:
                    sin_and_cos(j, half_rows(0), magnitude(j, half_rows(0)), early_sums)
                if half == 1:
                    rows = half_rows(1) if j < EARLY_TILES else all_rows
                    size = magnitude(j, rows)
                    if 1 < j <= GPSIMD_TILES:
                        scale_on_gpsimd(j - 1)
                    sin_and_cos(j, rows, size, late_sums)
                    if j == 0:
                        scale_on_gpsimd(0)
            if step == QUANTIZE_STEP:
                quantize_z(1)
            if step + 2 < len(units):
                second_product(*units[step + 2])
            if step >= TURN_STEP:
                turn_back_and_add(*gpsimd_halves[step - TURN_STEP])

        turned_so_far = len(units) + 1 - TURN_STEP
        for i in range(turned_so_far, len(gpsimd_halves) + 1):
            j, half = gpsimd_halves[i - 1]
            if i < len(gpsimd_halves):
                turn_back_and_add(*gpsimd_halves[i])
            store(j, half, on_vector=(j < GPSIMD_TILES - 1))
        for j in range(GPSIMD_TILES, TILES):
            scale_cos_on_vector(j)
            for half in range(2):
                combine_on_vector(j, half)
                turn_back(j, half)
        for j in range(GPSIMD_TILES, TILES):
            for half in range(2):
                store(j, half, on_vector=(j == LAST_TILE and half == 0))
